import numpy as np
import ml_dtypes


def mxq(x, axis, fmt="e4m3"):
    dtype, down = {"e4m3": (ml_dtypes.float8_e4m3fn, 7), "e5m2": (ml_dtypes.float8_e5m2, 14)}[fmt]
    v = np.moveaxis(np.asarray(x, np.float32).astype(ml_dtypes.bfloat16).astype(np.float64), axis, -1)
    blocks = v.reshape(v.shape[:-1] + (-1, 32))
    amax = np.abs(blocks).max(-1, keepdims=True)
    byte = np.maximum(np.where(amax > 0, np.frexp(amax)[1] - 1 + 127, 0) - down, 1)
    scale = np.exp2(byte - 127.0)
    codes = (blocks / scale).astype(np.float32).astype(dtype).astype(np.float64)
    return np.moveaxis((codes * scale).reshape(v.shape), -1, axis)


WIDE = False


def mx_kscale(k):
    if not WIDE:
        return np.ones(k)
    levels = np.array([10, -10, 5, -5, 0])
    if k % 512:
        return np.exp2(np.random.permutation(np.resize(levels, k // 32))).repeat(32)
    a = np.empty((k // 512, 16))
    for p in range(k // 512):
        a[p, :8] = np.random.permutation(np.resize(levels, 8))
        for g in range(8):
            far = levels[np.abs(levels - a[p, g]) >= 10]
            a[p, g + 8] = far[np.random.randint(len(far))]
    return np.exp2(a.ravel()).repeat(32)


BF16 = ml_dtypes.bfloat16


def bf(x):
    return np.asarray(x, np.float32).astype(BF16)


def f64(x):
    return np.asarray(x).astype(np.float64)

def planes(Y):
    n, m = Y.shape
    b = f64(bf(Y)).reshape(n // 32, 32, m)
    amax = np.abs(b).max(1)
    byte = np.clip(np.where(amax > 0, np.frexp(amax)[1] - 1 + 127 - 7, 1), 1, 254)
    codes = (b * np.exp2(127.0 - byte)[:, None, :]).reshape(n, m).astype(np.float32).astype(ml_dtypes.float8_e4m3fn).view(np.uint8)
    words = codes.reshape(n // 512, 128, 4, m).transpose(0, 1, 3, 2)
    return np.ascontiguousarray(words), np.ascontiguousarray(byte.astype(np.uint8).reshape(n // 512, 16, m))


T, U, D, F, V = 64, 32, 1024, 512, 2048
BETA = 0.9


def setup_inputs():
    R = T * U
    s = mx_kscale(D)
    t = mx_kscale(R)
    spread = np.exp(0.8 * np.random.randn(V))
    enc = np.random.randn(T, D)
    pred = np.random.randn(U, D)
    joint = ((enc[:, None, :] + pred[None, :, :]) / np.sqrt(2.0)).reshape(R, D)
    hidden_w = np.random.randn(D, F) / np.sqrt(D)
    state_w = np.exp(0.3 * np.random.randn(R))
    slopes = 1.5 * np.random.randn(R, V) / np.sqrt(R) * spread[None, :]
    bottleneck = np.random.randn(F, V) / np.sqrt(F) * spread[None, :]
    penalty = 3.0 * np.exp(0.3 * np.random.randn(V))
    momentum = np.random.randn(F, V) * spread[None, :]
    return {"joint": bf(joint * s[None, :]), "hidden_w": bf(hidden_w / s[:, None]),
            "state_w": bf(state_w * t), "slopes": bf(slopes / t[:, None]),
            "bottleneck": bf(bottleneck), "penalty": bf(penalty), "momentum": bf(momentum)}


def reference(joint, hidden_w, state_w, slopes, bottleneck, penalty, momentum):
    a = mxq(f64(joint), 1, "e4m3") @ mxq(f64(hidden_w), 0, "e4m3")
    h = np.tanh(a) * f64(state_w)[:, None]
    g = mxq(h, 0, "e4m3").T @ mxq(f64(slopes), 0, "e4m3")
    g = g + f64(penalty)[None, :] * f64(bottleneck)
    y = BETA * f64(momentum) + g
    words, scales = planes(y.T)
    return y, words, scales

@@ -1,0 +1,404 @@
+from contextlib import ExitStack
+
+import concourse.mybir as mybir
+from concourse.masks import make_identity
+
+R, D, F, V = 2048, 1024, 512, 2048
+BETA = 0.9
+FLOPS = 2 * R * D * F + 2 * R * F * V
+
+F32 = mybir.dt.float32
+BF16 = mybir.dt.bfloat16
+U32 = mybir.dt.uint32
+I32 = mybir.dt.int32
+U8 = mybir.dt.uint8
+FP8X4 = mybir.dt.float8_e4m3fn_x4
+ALU = mybir.AluOpType
+ACT = mybir.ActivationFunctionType
+
+P = 128
+PACK = 4
+KP = P * PACK
+NG = R // KP
+NS = D // KP
+NC = V // KP
+NF = F // P
+VEC_COLS = [128,320,320,320, 0,128,0,64, 0,208,0,208, 0,208,0,96]
+
+
+def tile_transducer_bottleneck_gradient_momen_h3_kernel(
+    tc, joint, hidden_w, state_w, slopes, bottleneck, penalty, momentum, out_0, out_1, out_2
+):
+    nc = tc.nc
+    with ExitStack() as ctx:
+        keep = ctx.enter_context(tc.tile_pool(name="keep", bufs=1))
+        raw = ctx.enter_context(tc.tile_pool(name="raw", bufs=12))
+        work = ctx.enter_context(tc.tile_pool(name="work", bufs=2))
+        psum = ctx.enter_context(tc.psum_pool(name="psum", bufs=1))
+        ctx.enter_context(tc.manual_schedule())
+
+        def bank(i, shape):
+            return psum.tile(shape, F32, name="bank", tag="bank%d" % i)
+
+        def quantize(codes, scales, grouped):
+            nc.vector.quantize_mx(out=codes.bitcast(FP8X4), scales=scales, in_=grouped)
+
+        def interleave(copy, grouped, rows, lo, hi):
+            copy(
+                out=grouped[:, PACK * lo : PACK * hi].rearrange("p (c i j) -> p c j i", i=4, j=PACK),
+                in_=rows[:, :, lo:hi].rearrange("p j (c i) -> p c j i", i=4),
+            )
+
+        ident = keep.tile([P, P], F32, name="ident")
+        make_identity(nc, ident[:])
+        rows = keep.tile([P, KP], BF16, name="rows")
+        row_words = rows[:].bitcast(F32)
+        for u in range(2):
+            nc.scalar.activation(out=row_words[:, u * P : (u + 1) * P], in_=ident[:], func=ACT.Tanh, scale=0.0)
+
+        j_raw = [raw.tile([P, PACK, D], BF16, name="j_raw", tag="raw") for g in range(NG)]
+        w_raw = raw.tile([P, NS, PACK, F], BF16, name="w_raw", tag="raw")
+
+        def load_joint(g, t0, t1):
+            src = joint[g * KP : (g + 1) * KP, :].rearrange("(m t) d -> m t d", t=PACK)
+            nc.sync.dma_start(out=j_raw[g][:, t0:t1, :], in_=src[:, t0:t1, :])
+
+        def load_w(s):
+            src = hidden_w[s * KP : (s + 1) * KP, :].rearrange("(p j) f -> p j f", j=PACK)
+            nc.sync.dma_start(out=w_raw[:, s, :, :], in_=src)
+
+        s_raw, b_raw, m_raw = {}, {}, {}
+
+        def load_slopes(h, g, lo=0, hi=2):
+            if (h, g) not in s_raw:
+                s_raw[h, g] = raw.tile([P, PACK, 2 * KP], BF16, name="s_raw", tag="raw")
+            src = slopes[g * KP : (g + 1) * KP, KP * (2 * h + lo) : KP * (2 * h + hi)]
+            nc.sync.dma_start(out=s_raw[h, g][:, :, lo * KP : hi * KP], in_=src.rearrange("(p j) v -> p j v", j=PACK))
+
+        def load_state(tiles, src, h, lo=0, hi=2):
+            if h not in tiles:
+                tiles[h] = raw.tile([P, NF, 2 * KP], BF16, name="state_raw", tag="raw")
+            nc.sync.dma_start(
+                out=tiles[h][:, :, lo * KP : hi * KP],
+                in_=src[:, KP * (2 * h + lo) : KP * (2 * h + hi)].rearrange("(a p) v -> p a v", p=P),
+            )
+
+        load_w(0)
+        load_joint(0, 0, 2)
+        nc.sync.dma_start(out=rows[0:8, 0 : 2 * P], in_=penalty.rearrange("(c w) -> c w", w=2 * P))
+        nc.sync.dma_start(out=rows[8:12, :], in_=state_w.rearrange("(g w) -> g w", w=KP))
+        load_w(1)
+        load_joint(0, 2, 4)
+        load_slopes(0, 0, 0, 1)
+        load_state(b_raw, bottleneck, 0, 0, 1)
+        load_joint(1, 0, 2)
+        load_state(m_raw, momentum, 0, 0, 1)
+        load_joint(1, 2, 4)
+        load_slopes(0, 1, 0, 1)
+        load_joint(2, 0, 4)
+        load_slopes(0, 2, 0, 1)
+        load_joint(3, 0, 4)
+        load_slopes(0, 3, 0, 1)
+        load_slopes(0, 0, 1, 2)
+        load_slopes(0, 1, 1, 2)
+        load_state(b_raw, bottleneck, 0, 1, 2)
+        load_state(m_raw, momentum, 0, 1, 2)
+        load_slopes(0, 2, 1, 2)
+        load_slopes(0, 3, 1, 2)
+
+
+        w_codes = keep.tile([P, NS, F], U32, name="w_codes", align_bytes=64)
+        w_scales = keep.tile([P, NS, F], U8, name="w_scales", align_bytes=64)
+        h_codes = keep.tile([P, NG, F], U32, name="h_codes", align_bytes=64)
+        h_scales = keep.tile([P, NG, F], U8, name="h_scales", align_bytes=64)
+        y_scales = keep.tile([P, NC, F], U8, name="y_scales", align_bytes=64)
+        pen_cols = keep.tile([P, 8], F32, name="pen_cols")
+        w_grp, j_grp, j_codes, j_scales, tanh_a, h_grp = {}, {}, {}, {}, {}, {}
+        turn = [0, 0]
+
+        def turn_bank():
+            turn[0] += 1
+            return bank(2 + turn[0] % (3 if turn[0] <= 16 else 2), [P, 4, P])
+
+        def group_w(s, cut):
+            w_grp[s] = work.tile([P, PACK * F], BF16, name="w_grp", tag="grp", bufs=4, align_bytes=64)
+            interleave(nc.vector.tensor_copy, w_grp[s], w_raw[:, s, :, :], 0, cut)
+            if cut < F:
+                interleave(nc.scalar.copy, w_grp[s], w_raw[:, s, :, :], cut, F)
+
+        def turn_joint(g, t):
+            if t % 2 == 0:
+                j_grp[g, t // 2] = work.tile([P, 2, D], BF16, name="j_grp", bufs=2, align_bytes=64)
+            words = j_raw[g][:, t, :].bitcast(F32)
+            turned = turn_bank()
+            for s in range(NS):
+                for u in range(2):
+                    nc.tensor.transpose(turned[:, 2 * s + u, :], words[:, 2 * P * s + u : 2 * P * (s + 1) : 2], ident[:])
+            nc.scalar.copy(
+                out=j_grp[g, t // 2][:, t % 2, :].bitcast(F32).rearrange("p (s r u) -> p s r u", s=NS, u=2),
+                in_=turned[:].rearrange("p (s u) r -> p s r u", u=2),
+            )
+
+        def quantize_joint(g, a):
+            j_codes[g, a] = work.tile([P, 4 * P], U32, name="j_codes", bufs=4, align_bytes=64)
+            j_scales[g, a] = work.tile([P, 4 * P], U8, name="j_scales", bufs=4, align_bytes=64)
+            quantize(j_codes[g, a][:], j_scales[g, a][:], j_grp[g, a][:].rearrange("p t d -> p (t d)"))
+
+        def hidden(g, q):
+            turn[1] += 1
+            acc = bank(5 + turn[1] % 3, [P, PACK, P])
+            cols = slice(q * P, (q + 1) * P)
+            for t in range(PACK):
+                for s in range(NS):
+                    rs = slice((2 * (t % 2) + s) * P, (2 * (t % 2) + s + 1) * P)
+                    nc.tensor.matmul_mx(
+                        out=acc[:, t, :],
+                        lhsT=j_codes[g, t // 2][:, rs].bitcast(FP8X4),
+                        lhsT_scale=j_scales[g, t // 2][:, rs],
+                        rhs=w_codes[:, s, cols].bitcast(FP8X4),
+                        rhs_scale=w_scales[:, s, cols],
+                        start=(s == 0),
+                        stop=(s == NS - 1),
+                    )
+            tanh_a[g, q] = work.tile([P, P, PACK], F32, name="tanh_a", bufs=3)
+            nc.scalar.activation(out=tanh_a[g, q][:], in_=acc[:].rearrange("p t f -> p f t"), func=ACT.Tanh)
+
+        def weigh(g, q):
+            if q == 0:
+                h_grp[g] = work.tile([P, PACK * F], BF16, name="h_grp", bufs=2, align_bytes=64)
+            weights = vec[:].bitcast(BF16)[:, 1:3, 2 * (8 + g) : 2 * (9 + g)]
+            nc.vector.tensor_tensor(
+                out=h_grp[g][:, q * KP : (q + 1) * KP].rearrange("p (f u e) -> p f u e", u=2, e=2),
+                in0=tanh_a[g, q][:].rearrange("p f (u e) -> p f u e", u=2),
+                in1=weights.rearrange("p u (o e) -> p o u e", o=1).to_broadcast([P, P, 2, 2]),
+                op=ALU.mult,
+            )
+
+        def quantize_h(g):
+            quantize(h_codes[:, g, :], h_scales[:, g, :], h_grp[g][:])
+
+        s_grp, s_codes, s_scales, pen, prod, rest, g_acc, y, y_bf, y_turned, y_grp = ({} for i in range(11))
+
+        def group_slopes(c, g, part):
+            if (c, g) not in s_grp:
+                s_grp[c, g] = work.tile([P, PACK * KP], BF16, name="s_grp", tag="grp", bufs=4, align_bytes=64)
+            src = s_raw[c // 2, g][:, :, (c % 2) * KP : (c % 2 + 1) * KP]
+            cut = VEC_COLS[4 * c + g]
+            if part == "scalar" and cut < KP:
+                interleave(nc.scalar.copy, s_grp[c, g], src, cut, KP)
+            if part == "vector" and cut > 0:
+                interleave(nc.vector.tensor_copy, s_grp[c, g], src, 0, cut)
+            if part == "gpsimd" and cut > 0:
+                nc.gpsimd.tensor_scalar(
+                    out=s_grp[c, g][:, 0 : PACK * cut].rearrange("p (v j) -> p v j", j=PACK),
+                    in0=src[:, :, 0:cut].rearrange("p j v -> p v j"),
+                    scalar1=1.0, scalar2=0.0, op0=ALU.mult, op1=ALU.add,
+                )
+
+        def quantize_slopes(c, g):
+            if g == 0:
+                s_codes[c] = work.tile([P, NG, KP], U32, name="s_codes", align_bytes=64)
+                s_scales[c] = work.tile([P, NG, KP], U8, name="s_scales", align_bytes=64)
+            quantize(s_codes[c][:, g, :], s_scales[c][:, g, :], s_grp[c, g][:])
+
+        def spread_penalty(h):
+            pen[h] = bank((1, 4)[h], [P, 4, P])
+            for i in range(4):
+                col = pen_cols[:, 4 * h + i : 4 * h + i + 1]
+                nc.tensor.transpose(pen[h][:, i, :], col.to_broadcast([P, P]), ident[:])
+
+        def penalty_term(c, a):
+            cols = slice((c % 2) * KP, (c % 2 + 1) * KP)
+            prod[c, a] = work.tile([P, KP], F32, name="prod", bufs=2)
+            nc.vector.tensor_tensor(
+                out=prod[c, a][:],
+                in0=b_raw[c // 2][:, a, cols],
+                in1=pen[c // 2][:].rearrange("p i w -> p (i w)").bitcast(BF16)[:, cols],
+                op=ALU.mult,
+            )
+
+        def momentum_term(c, a):
+            cols = slice((c % 2) * KP, (c % 2 + 1) * KP)
+            rest[c, a] = work.tile([P, KP], F32, name="rest", bufs=6)
+            nc.vector.scalar_tensor_tensor(
+                out=rest[c, a][:], in0=m_raw[c // 2][:, a, cols], scalar=BETA, in1=prod[c, a][:],
+                op0=ALU.mult, op1=ALU.add,
+            )
+
+        def gradient(c, a, g):
+            if g == 0:
+                g_acc[c, a] = bank((5, 6, 7, 0)[a], [P, KP])
+            cols = slice(a * P, (a + 1) * P)
+            nc.tensor.matmul_mx(
+                out=g_acc[c, a][:],
+                lhsT=h_codes[:, g, cols].bitcast(FP8X4),
+                lhsT_scale=h_scales[:, g, cols],
+                rhs=s_codes[c][:, g, :].bitcast(FP8X4),
+                rhs_scale=s_scales[c][:, g, :],
+                start=(g == 0),
+                stop=(g == NG - 1),
+            )
+
+        def finish(c, a):
+            y[c, a] = work.tile([P, KP], F32, name="y", bufs=6)
+            nc.vector.tensor_tensor(out=y[c, a][:], in0=g_acc[c, a][:], in1=rest[c, a][:], op=ALU.add)
+            nc.sync.dma_start(out=out_0[a * P : (a + 1) * P, c * KP : (c + 1) * KP], in_=y[c, a][:])
+
+        def round_y(c, a, copy=nc.scalar.copy):
+            y_bf[c, a] = work.tile([P, 2, P, 2], BF16, name="y_bf", bufs=3)
+            copy(out=y_bf[c, a][:], in_=y[c, a][:].rearrange("f (p u e) -> f u p e", u=2, e=2))
+
+        def turn_y(c, b):
+            turned = y_turned[c, b] = turn_bank()
+            for a in range(2):
+                words = y_bf[c, 2 * b + a][:].rearrange("f u p e -> f (u p e)").bitcast(F32)
+                for u in range(2):
+                    nc.tensor.transpose(turned[:, 2 * a + u, :], words[:, u * P : (u + 1) * P], ident[:])
+
+        def group_y(c, b, copy=nc.scalar.copy):
+            if b == 0:
+                y_grp[c] = work.tile([P, PACK * F], BF16, name="y_grp", align_bytes=64)
+            copy(
+                out=y_grp[c][:].bitcast(F32)[:, b * KP : (b + 1) * KP].rearrange("p (a f u) -> p a f u", a=2, u=2),
+                in_=y_turned[c, b][:].rearrange("p (a u) f -> p a f u", u=2),
+            )
+
+        def quantize_y(c, lo, hi):
+            y_codes = work.tile([P, F], U32, name="y_codes", bufs=3, align_bytes=64)
+            quantize(y_codes[:, lo:hi], y_scales[:, c, lo:hi], y_grp[c][:, PACK * lo : PACK * hi])
+            dst = out_1[c, :, :, :].rearrange("p m t -> p (m t)").bitcast(I32)
+            nc.sync.dma_start(out=dst[:, lo:hi], in_=y_codes[:, lo:hi].bitcast(I32))
+
+        group_w(0, 336)
+        turn_joint(0, 0)
+        turn_joint(0, 1)
+        vec = bank(0, [P, 3, P])
+        nc.tensor.transpose(vec[:, 0, :], row_words[:, 0:P], ident[:])
+        for u in range(2):
+            nc.tensor.transpose(vec[:, 1 + u, :], row_words[:, u : 2 * P : 2], ident[:])
+        nc.scalar.copy(out=pen_cols[:], in_=vec[:, 0, 0:8])
+        quantize(w_codes[:, 0, :], w_scales[:, 0, :], w_grp[0][:])
+        group_w(1, 336)
+        quantize_joint(0, 0)
+        spread_penalty(0)
+        turn_joint(0, 2)
+        turn_joint(0, 3)
+        quantize(w_codes[:, 1, :], w_scales[:, 1, :], w_grp[1][:])
+        group_slopes(0, 0, "vector")
+        group_slopes(0, 0, "scalar")
+        quantize_joint(0, 1)
+        penalty_term(0, 0)
+        penalty_term(0, 1)
+        quantize_slopes(0, 0)
+
+        for i in range(2 * NG):
+            g, a = divmod(i, 2)
+            if g + 1 < NG:
+                turn_joint(g + 1, 2 * a)
+                turn_joint(g + 1, 2 * a + 1)
+            if i == 6:
+                spread_penalty(1)
+            hidden(g, 2 * a)
+            hidden(g, 2 * a + 1)
+            if i in (1, 3, 5):
+                group_slopes(0, (i + 1) // 2, "scalar")
+            if i >= 6:
+                group_slopes(1, i - 6, "scalar")
+            if i == 0:
+                momentum_term(0, 0)
+                momentum_term(0, 1)
+            if g + 1 < NG:
+                quantize_joint(g + 1, a)
+            if g > 0 and a == 0:
+                quantize_h(g - 1)
+            if i == 0:
+                penalty_term(0, 2)
+                penalty_term(0, 3)
+            if i == 1:
+                momentum_term(0, 2)
+                momentum_term(0, 3)
+            if i in (2, 4, 6):
+                quantize_slopes(0, i // 2)
+            weigh(g, 2 * a)
+            weigh(g, 2 * a + 1)
+            if i in (1, 3, 5):
+                group_slopes(0, (i + 1) // 2, "vector")
+            if i >= 6:
+                group_slopes(1, i - 6, "vector")
+        load_slopes(1, 0)
+        load_slopes(1, 1)
+        load_state(b_raw, bottleneck, 1)
+        load_state(m_raw, momentum, 1)
+        load_slopes(1, 2)
+        load_slopes(1, 3)
+        quantize_h(NG - 1)
+        for a in range(NF):
+            for g in range(NG):
+                gradient(0, a, g)
+
+        for c in range(NC - 1):
+            n = c + 1
+            group_slopes(n, 2, "scalar")
+            penalty_term(n, 0)
+            penalty_term(n, 1)
+            finish(c, 0)
+            finish(c, 1)
+            round_y(c, 0)
+            round_y(c, 1)
+            turn_y(c, 0)
+            group_slopes(n, 3, "scalar")
+            momentum_term(n, 0)
+            momentum_term(n, 1)
+            group_slopes(n, 3, "vector")
+            if c > 0:
+                quantize_y(c - 1, 0, F)
+            quantize_slopes(n, 0)
+            quantize_slopes(n, 1)
+            for g in range(2):
+                for a in range(2):
+                    gradient(n, a, g)
+            penalty_term(n, 2)
+            penalty_term(n, 3)
+            finish(c, 2)
+            finish(c, 3)
+            group_y(c, 0)
+            round_y(c, 2)
+            round_y(c, 3)
+            for g in range(2):
+                for a in range(2, 4):
+                    gradient(n, a, g)
+            if n + 1 < NC:
+                group_slopes(n + 1, 0, "scalar")
+                group_slopes(n + 1, 1, "scalar")
+            for g in range(2, 4):
+                quantize_slopes(n, g)
+                for a in range(NF):
+                    gradient(n, a, g)
+                if g == 2:
+                    turn_y(c, 1)
+            group_y(c, 1)
+            momentum_term(n, 2)
+            momentum_term(n, 3)
+            if n + 1 < NC:
+                group_slopes(n + 1, 1, "vector")
+        c = NC - 1
+        for a in range(NF):
+            finish(c, a)
+            if a == 1:
+                quantize_y(c - 1, 0, F)
+            if a < 3:
+                round_y(c, a)
+            if a == 1:
+                turn_y(c, 0)
+        group_y(c, 0)
+        round_y(c, 3, nc.vector.tensor_copy)
+        turn_y(c, 1)
+        quantize_y(c, 0, F // 2)
+        group_y(c, 1, nc.vector.tensor_copy)
+        quantize_y(c, F // 2, F)
+
+        for q in range(4):
+            nc.sync.dma_start(
+                out=out_2[:, 4 * q : 4 * q + 4, :].rearrange("g r m -> r g m").bitcast(I32),
+                in_=y_scales[32 * q : 32 * q + 4, :, :].bitcast(I32),
+            )

@@ -33,6 +33,7 @@ def tile_transducer_bottleneck_gradient_momen_h3_kernel(
     with ExitStack() as ctx:
         keep = ctx.enter_context(tc.tile_pool(name="keep", bufs=1))
         raw = ctx.enter_context(tc.tile_pool(name="raw", bufs=12))
+        wide = ctx.enter_context(tc.tile_pool(name="wide", bufs=1))
         work = ctx.enter_context(tc.tile_pool(name="work", bufs=2))
         psum = ctx.enter_context(tc.psum_pool(name="psum", bufs=1))
         ctx.enter_context(tc.manual_schedule())
@@ -56,55 +57,58 @@ def tile_transducer_bottleneck_gradient_momen_h3_kernel(
         for u in range(2):
             nc.scalar.activation(out=row_words[:, u * P : (u + 1) * P], in_=ident[:], func=ACT.Tanh, scale=0.0)
 
-        j_raw = [raw.tile([P, PACK, D], BF16, name="j_raw", tag="raw") for g in range(NG)]
-        w_raw = raw.tile([P, NS, PACK, F], BF16, name="w_raw", tag="raw")
+        j_raw, w_raw, s_raw, b_raw, m_raw = {}, {}, {}, {}, {}
 
-        def load_joint(g, t0, t1):
+        def load_joint(g, a):
+            j_raw[g, a] = raw.tile([P, 2, D], BF16, name="j_raw", tag="raw")
             src = joint[g * KP : (g + 1) * KP, :].rearrange("(m t) d -> m t d", t=PACK)
-            nc.sync.dma_start(out=j_raw[g][:, t0:t1, :], in_=src[:, t0:t1, :])
+            nc.sync.dma_start(out=j_raw[g, a][:], in_=src[:, 2 * a : 2 * a + 2, :])
 
         def load_w(s):
+            w_raw[s] = raw.tile([P, PACK, F], BF16, name="w_raw", tag="raw")
             src = hidden_w[s * KP : (s + 1) * KP, :].rearrange("(p j) f -> p j f", j=PACK)
-            nc.sync.dma_start(out=w_raw[:, s, :, :], in_=src)
+            nc.sync.dma_start(out=w_raw[s][:], in_=src)
 
-        s_raw, b_raw, m_raw = {}, {}, {}
+        def load_columns(tiles, key, src, c, n):
+            if n == 1:
+                t = raw.tile([P, 4, KP], BF16, name="narrow", tag="raw")
+            else:
+                t = wide.tile([P, 4, n * KP], BF16, name="wide%d" % len(wides))
+                wides.append(t)
+            nc.sync.dma_start(out=t[:], in_=src[:, :, c * KP : (c + n) * KP])
+            for i in range(n):
+                tiles[(c + i,) + key] = t[:, :, i * KP : (i + 1) * KP]
 
-        def load_slopes(h, g, lo=0, hi=2):
-            if (h, g) not in s_raw:
-                s_raw[h, g] = raw.tile([P, PACK, 2 * KP], BF16, name="s_raw", tag="raw")
-            src = slopes[g * KP : (g + 1) * KP, KP * (2 * h + lo) : KP * (2 * h + hi)]
-            nc.sync.dma_start(out=s_raw[h, g][:, :, lo * KP : hi * KP], in_=src.rearrange("(p j) v -> p j v", j=PACK))
+        wides = []
 
-        def load_state(tiles, src, h, lo=0, hi=2):
-            if h not in tiles:
-                tiles[h] = raw.tile([P, NF, 2 * KP], BF16, name="state_raw", tag="raw")
-            nc.sync.dma_start(
-                out=tiles[h][:, :, lo * KP : hi * KP],
-                in_=src[:, KP * (2 * h + lo) : KP * (2 * h + hi)].rearrange("(a p) v -> p a v", p=P),
-            )
+        def load_slopes(c, g, n=1):
+            load_columns(s_raw, (g,), slopes[g * KP : (g + 1) * KP, :].rearrange("(p j) v -> p j v", j=PACK), c, n)
+
+        def load_state(c, n=1):
+            load_columns(b_raw, (), bottleneck.rearrange("(a p) v -> p a v", p=P), c, n)
+
+        def load_momentum(c, n=1):
+            load_columns(m_raw, (), momentum.rearrange("(a p) v -> p a v", p=P), c, n)
 
         load_w(0)
-        load_joint(0, 0, 2)
+        load_joint(0, 0)
         nc.sync.dma_start(out=rows[0:8, 0 : 2 * P], in_=penalty.rearrange("(c w) -> c w", w=2 * P))
         nc.sync.dma_start(out=rows[8:12, :], in_=state_w.rearrange("(g w) -> g w", w=KP))
         load_w(1)
-        load_joint(0, 2, 4)
-        load_slopes(0, 0, 0, 1)
-        load_state(b_raw, bottleneck, 0, 0, 1)
-        load_joint(1, 0, 2)
-        load_state(m_raw, momentum, 0, 0, 1)
-        load_joint(1, 2, 4)
-        load_slopes(0, 1, 0, 1)
-        load_joint(2, 0, 4)
-        load_slopes(0, 2, 0, 1)
-        load_joint(3, 0, 4)
-        load_slopes(0, 3, 0, 1)
-        load_slopes(0, 0, 1, 2)
-        load_slopes(0, 1, 1, 2)
-        load_state(b_raw, bottleneck, 0, 1, 2)
-        load_state(m_raw, momentum, 0, 1, 2)
-        load_slopes(0, 2, 1, 2)
-        load_slopes(0, 3, 1, 2)
+        load_joint(0, 1)
+        load_slopes(0, 0)
+        load_state(0)
+        load_joint(1, 0)
+        load_momentum(0)
+        load_joint(1, 1)
+        load_slopes(0, 1)
+        load_joint(2, 0)
+        load_joint(2, 1)
+        later = [
+            lambda: load_slopes(0, 2), lambda: load_joint(3, 0), lambda: load_joint(3, 1), lambda: load_slopes(0, 3),
+            lambda: load_slopes(1, 0), lambda: load_slopes(1, 1), lambda: load_state(1), lambda: load_momentum(1),
+            lambda: load_slopes(1, 2), lambda: load_slopes(1, 3),
+        ]
 
 
         w_codes = keep.tile([P, NS, F], U32, name="w_codes", align_bytes=64)
@@ -122,14 +126,14 @@ def tile_transducer_bottleneck_gradient_momen_h3_kernel(
 
         def group_w(s, cut):
             w_grp[s] = work.tile([P, PACK * F], BF16, name="w_grp", tag="grp", bufs=4, align_bytes=64)
-            interleave(nc.vector.tensor_copy, w_grp[s], w_raw[:, s, :, :], 0, cut)
+            interleave(nc.vector.tensor_copy, w_grp[s], w_raw[s][:], 0, cut)
             if cut < F:
-                interleave(nc.scalar.copy, w_grp[s], w_raw[:, s, :, :], cut, F)
+                interleave(nc.scalar.copy, w_grp[s], w_raw[s][:], cut, F)
 
         def turn_joint(g, t):
             if t % 2 == 0:
                 j_grp[g, t // 2] = work.tile([P, 2, D], BF16, name="j_grp", bufs=2, align_bytes=64)
-            words = j_raw[g][:, t, :].bitcast(F32)
+            words = j_raw[g, t // 2][:, t % 2, :].bitcast(F32)
             turned = turn_bank()
             for s in range(NS):
                 for u in range(2):
@@ -182,7 +186,7 @@ def tile_transducer_bottleneck_gradient_momen_h3_kernel(
         def group_slopes(c, g, part):
             if (c, g) not in s_grp:
                 s_grp[c, g] = work.tile([P, PACK * KP], BF16, name="s_grp", tag="grp", bufs=4, align_bytes=64)
-            src = s_raw[c // 2, g][:, :, (c % 2) * KP : (c % 2 + 1) * KP]
+            src = s_raw[c, g]
             cut = VEC_COLS[4 * c + g]
             if part == "scalar" and cut < KP:
                 interleave(nc.scalar.copy, s_grp[c, g], src, cut, KP)
@@ -212,7 +216,7 @@ def tile_transducer_bottleneck_gradient_momen_h3_kernel(
             prod[c, a] = work.tile([P, KP], F32, name="prod", bufs=2)
             nc.vector.tensor_tensor(
                 out=prod[c, a][:],
-                in0=b_raw[c // 2][:, a, cols],
+                in0=b_raw[c,][:, a, :],
                 in1=pen[c // 2][:].rearrange("p i w -> p (i w)").bitcast(BF16)[:, cols],
                 op=ALU.mult,
             )
@@ -221,7 +225,7 @@ def tile_transducer_bottleneck_gradient_momen_h3_kernel(
             cols = slice((c % 2) * KP, (c % 2 + 1) * KP)
             rest[c, a] = work.tile([P, KP], F32, name="rest", bufs=6)
             nc.vector.scalar_tensor_tensor(
-                out=rest[c, a][:], in0=m_raw[c // 2][:, a, cols], scalar=BETA, in1=prod[c, a][:],
+                out=rest[c, a][:], in0=m_raw[c,][:, a, :], scalar=BETA, in1=prod[c, a][:],
                 op0=ALU.mult, op1=ALU.add,
             )
 
@@ -293,6 +297,12 @@ def tile_transducer_bottleneck_gradient_momen_h3_kernel(
 
         for i in range(2 * NG):
             g, a = divmod(i, 2)
+            if i == 1:
+                for f in later[:5]:
+                    f()
+            if i == 3:
+                for f in later[5:]:
+                    f()
             if g + 1 < NG:
                 turn_joint(g + 1, 2 * a)
                 turn_joint(g + 1, 2 * a + 1)
@@ -325,12 +335,12 @@ def tile_transducer_bottleneck_gradient_momen_h3_kernel(
                 group_slopes(0, (i + 1) // 2, "vector")
             if i >= 6:
                 group_slopes(1, i - 6, "vector")
-        load_slopes(1, 0)
-        load_slopes(1, 1)
-        load_state(b_raw, bottleneck, 1)
-        load_state(m_raw, momentum, 1)
-        load_slopes(1, 2)
-        load_slopes(1, 3)
+        load_slopes(2, 0, 2)
+        load_slopes(2, 1, 2)
+        load_state(2, 2)
+        load_momentum(2, 2)
+        load_slopes(2, 2, 2)
+        load_slopes(2, 3, 2)
         quantize_h(NG - 1)
         for a in range(NF):
             for g in range(NG):

@@ -23,7 +23,10 @@ NG = R // KP
 NS = D // KP
 NC = V // KP
 NF = F // P
-VEC_COLS = [128,320,320,320, 0,128,0,64, 0,208,0,208, 0,208,0,96]
+REUSE = [0, 1, 2, 3, 6, 4, 8, 5, 10, 11]
+VEC_COLS = [512,224,224,64, 0,0,0,0, 0,0,96,0, 64,0,0,0]
+W_VEC_COLS = 336
+SIDE_COLS = [0,288,288,448, 0,288,0,288, 0,288,0,288, 0,288,0,288]
 
 
 def tile_transducer_bottleneck_gradient_momen_h3_kernel(
@@ -32,7 +35,7 @@ def tile_transducer_bottleneck_gradient_momen_h3_kernel(
     nc = tc.nc
     with ExitStack() as ctx:
         keep = ctx.enter_context(tc.tile_pool(name="keep", bufs=1))
-        raw = ctx.enter_context(tc.tile_pool(name="raw", bufs=12))
+        raw = ctx.enter_context(tc.tile_pool(name="raw", bufs=1))
         wide = ctx.enter_context(tc.tile_pool(name="wide", bufs=1))
         work = ctx.enter_context(tc.tile_pool(name="work", bufs=2))
         psum = ctx.enter_context(tc.psum_pool(name="psum", bufs=1))
@@ -51,27 +54,31 @@ def tile_transducer_bottleneck_gradient_momen_h3_kernel(
             )
 
         ident = keep.tile([P, P], F32, name="ident")
-        make_identity(nc, ident[:])
         rows = keep.tile([P, KP], BF16, name="rows")
         row_words = rows[:].bitcast(F32)
+        nc.gpsimd.memset(row_words[0:64, :], 0.0)
+        make_identity(nc, ident[:])
         for u in range(2):
-            nc.scalar.activation(out=row_words[:, u * P : (u + 1) * P], in_=ident[:], func=ACT.Tanh, scale=0.0)
+            nc.scalar.activation(
+                out=row_words[64:P, u * P : (u + 1) * P], in_=ident[64:P, :], func=ACT.Tanh, scale=0.0
+            )
 
+        slots = list(range(12)) + REUSE
         j_raw, w_raw, s_raw, b_raw, m_raw = {}, {}, {}, {}, {}
 
         def load_joint(g, a):
-            j_raw[g, a] = raw.tile([P, 2, D], BF16, name="j_raw", tag="raw")
+            j_raw[g, a] = raw.tile([P, 2, D], BF16, name="j_raw", tag="raw%d" % slots.pop(0))
             src = joint[g * KP : (g + 1) * KP, :].rearrange("(m t) d -> m t d", t=PACK)
             nc.sync.dma_start(out=j_raw[g, a][:], in_=src[:, 2 * a : 2 * a + 2, :])
 
         def load_w(s):
-            w_raw[s] = raw.tile([P, PACK, F], BF16, name="w_raw", tag="raw")
+            w_raw[s] = raw.tile([P, PACK, F], BF16, name="w_raw", tag="raw%d" % slots.pop(0))
             src = hidden_w[s * KP : (s + 1) * KP, :].rearrange("(p j) f -> p j f", j=PACK)
             nc.sync.dma_start(out=w_raw[s][:], in_=src)
 
         def load_columns(tiles, key, src, c, n):
             if n == 1:
-                t = raw.tile([P, 4, KP], BF16, name="narrow", tag="raw")
+                t = raw.tile([P, 4, KP], BF16, name="narrow", tag="raw%d" % slots.pop(0))
             else:
                 t = wide.tile([P, 4, n * KP], BF16, name="wide%d" % len(wides))
                 wides.append(t)
@@ -96,18 +103,25 @@ def tile_transducer_bottleneck_gradient_momen_h3_kernel(
         nc.sync.dma_start(out=rows[8:12, :], in_=state_w.rearrange("(g w) -> g w", w=KP))
         load_w(1)
         load_joint(0, 1)
-        load_slopes(0, 0)
         load_state(0)
-        load_joint(1, 0)
         load_momentum(0)
+        load_joint(1, 0)
+        load_slopes(0, 0)
         load_joint(1, 1)
         load_slopes(0, 1)
         load_joint(2, 0)
         load_joint(2, 1)
         later = [
-            lambda: load_slopes(0, 2), lambda: load_joint(3, 0), lambda: load_joint(3, 1), lambda: load_slopes(0, 3),
-            lambda: load_slopes(1, 0), lambda: load_slopes(1, 1), lambda: load_state(1), lambda: load_momentum(1),
-            lambda: load_slopes(1, 2), lambda: load_slopes(1, 3),
+            lambda: load_slopes(0, 2),
+            lambda: load_joint(3, 0),
+            lambda: load_joint(3, 1),
+            lambda: load_slopes(0, 3),
+            lambda: load_slopes(1, 0),
+            lambda: load_state(1),
+            lambda: load_slopes(1, 1),
+            lambda: load_momentum(1),
+            lambda: load_slopes(1, 2),
+            lambda: load_slopes(1, 3),
         ]
 
 
@@ -125,7 +139,7 @@ def tile_transducer_bottleneck_gradient_momen_h3_kernel(
             return bank(2 + turn[0] % (3 if turn[0] <= 16 else 2), [P, 4, P])
 
         def group_w(s, cut):
-            w_grp[s] = work.tile([P, PACK * F], BF16, name="w_grp", tag="grp", bufs=4, align_bytes=64)
+            w_grp[s] = work.tile([P, PACK * F], BF16, name="w_grp", tag="grp", bufs=3, align_bytes=64)
             interleave(nc.vector.tensor_copy, w_grp[s], w_raw[s][:], 0, cut)
             if cut < F:
                 interleave(nc.scalar.copy, w_grp[s], w_raw[s][:], cut, F)
@@ -164,7 +178,7 @@ def tile_transducer_bottleneck_gradient_momen_h3_kernel(
                         start=(s == 0),
                         stop=(s == NS - 1),
                     )
-            tanh_a[g, q] = work.tile([P, P, PACK], F32, name="tanh_a", bufs=3)
+            tanh_a[g, q] = work.tile([P, P, PACK], F32, name="tanh_a", bufs=4)
             nc.scalar.activation(out=tanh_a[g, q][:], in_=acc[:].rearrange("p t f -> p f t"), func=ACT.Tanh)
 
         def weigh(g, q):
@@ -184,18 +198,22 @@ def tile_transducer_bottleneck_gradient_momen_h3_kernel(
         s_grp, s_codes, s_scales, pen, prod, rest, g_acc, y, y_bf, y_turned, y_grp = ({} for i in range(11))
 
         def group_slopes(c, g, part):
+            side = c == 0 or g % 2 == 1
             if (c, g) not in s_grp:
-                s_grp[c, g] = work.tile([P, PACK * KP], BF16, name="s_grp", tag="grp", bufs=4, align_bytes=64)
+                s_grp[c, g] = work.tile(
+                    [P, PACK * KP], BF16, name="s_grp", tag="side" if side else "grp", bufs=1 if side else 3, align_bytes=64
+                )
             src = s_raw[c, g]
-            cut = VEC_COLS[4 * c + g]
-            if part == "scalar" and cut < KP:
-                interleave(nc.scalar.copy, s_grp[c, g], src, cut, KP)
-            if part == "vector" and cut > 0:
-                interleave(nc.vector.tensor_copy, s_grp[c, g], src, 0, cut)
-            if part == "gpsimd" and cut > 0:
+            lo = SIDE_COLS[4 * c + g]
+            hi = lo + VEC_COLS[4 * c + g]
+            if part == "scalar" and hi < KP:
+                interleave(nc.scalar.copy, s_grp[c, g], src, hi, KP)
+            if part == "vector" and hi > lo:
+                interleave(nc.vector.tensor_copy, s_grp[c, g], src, lo, hi)
+            if part == "gpsimd" and lo > 0:
                 nc.gpsimd.tensor_scalar(
-                    out=s_grp[c, g][:, 0 : PACK * cut].rearrange("p (v j) -> p v j", j=PACK),
-                    in0=src[:, :, 0:cut].rearrange("p j v -> p v j"),
+                    out=s_grp[c, g][:, 0 : PACK * lo].rearrange("p (v j) -> p v j", j=PACK),
+                    in0=src[:, :, 0:lo].rearrange("p j v -> p v j"),
                     scalar1=1.0, scalar2=0.0, op0=ALU.mult, op1=ALU.add,
                 )
 
@@ -223,7 +241,7 @@ def tile_transducer_bottleneck_gradient_momen_h3_kernel(
 
         def momentum_term(c, a):
             cols = slice((c % 2) * KP, (c % 2 + 1) * KP)
-            rest[c, a] = work.tile([P, KP], F32, name="rest", bufs=6)
+            rest[c, a] = work.tile([P, KP], F32, name="rest", bufs=8)
             nc.vector.scalar_tensor_tensor(
                 out=rest[c, a][:], in0=m_raw[c,][:, a, :], scalar=BETA, in1=prod[c, a][:],
                 op0=ALU.mult, op1=ALU.add,
@@ -249,7 +267,7 @@ def tile_transducer_bottleneck_gradient_momen_h3_kernel(
             nc.sync.dma_start(out=out_0[a * P : (a + 1) * P, c * KP : (c + 1) * KP], in_=y[c, a][:])
 
         def round_y(c, a, copy=nc.scalar.copy):
-            y_bf[c, a] = work.tile([P, 2, P, 2], BF16, name="y_bf", bufs=3)
+            y_bf[c, a] = work.tile([P, 2, P, 2], BF16, name="y_bf", bufs=4)
             copy(out=y_bf[c, a][:], in_=y[c, a][:].rearrange("f (p u e) -> f u p e", u=2, e=2))
 
         def turn_y(c, b):
@@ -267,13 +285,28 @@ def tile_transducer_bottleneck_gradient_momen_h3_kernel(
                 in_=y_turned[c, b][:].rearrange("p (a u) f -> p a f u", u=2),
             )
 
+        def turn_last(c, a, copy):
+            turned = bank(2 + a % 2, [P, 2, P])
+            words = y_bf[c, a][:].rearrange("f u p e -> f (u p e)").bitcast(F32)
+            for u in range(2):
+                nc.tensor.transpose(turned[:, u, :], words[:, u * P : (u + 1) * P], ident[:])
+            copy(
+                out=y_grp[c][:].bitcast(F32)[:, a * 2 * P : (a + 1) * 2 * P].rearrange("p (f u) -> p f u", u=2),
+                in_=turned[:].rearrange("p u f -> p f u"),
+            )
+
         def quantize_y(c, lo, hi):
             y_codes = work.tile([P, F], U32, name="y_codes", bufs=3, align_bytes=64)
             quantize(y_codes[:, lo:hi], y_scales[:, c, lo:hi], y_grp[c][:, PACK * lo : PACK * hi])
             dst = out_1[c, :, :, :].rearrange("p m t -> p (m t)").bitcast(I32)
             nc.sync.dma_start(out=dst[:, lo:hi], in_=y_codes[:, lo:hi].bitcast(I32))
 
-        group_w(0, 336)
+        def terms(j, which):
+            c, b = divmod(j, 2)
+            for a in (2 * b, 2 * b + 1):
+                which(c, a)
+
+        group_w(0, W_VEC_COLS)
         turn_joint(0, 0)
         turn_joint(0, 1)
         vec = bank(0, [P, 3, P])
@@ -282,133 +315,144 @@ def tile_transducer_bottleneck_gradient_momen_h3_kernel(
             nc.tensor.transpose(vec[:, 1 + u, :], row_words[:, u : 2 * P : 2], ident[:])
         nc.scalar.copy(out=pen_cols[:], in_=vec[:, 0, 0:8])
         quantize(w_codes[:, 0, :], w_scales[:, 0, :], w_grp[0][:])
-        group_w(1, 336)
+        group_w(1, W_VEC_COLS)
         quantize_joint(0, 0)
         spread_penalty(0)
         turn_joint(0, 2)
         turn_joint(0, 3)
         quantize(w_codes[:, 1, :], w_scales[:, 1, :], w_grp[1][:])
-        group_slopes(0, 0, "vector")
-        group_slopes(0, 0, "scalar")
+        terms(0, penalty_term)
         quantize_joint(0, 1)
-        penalty_term(0, 0)
-        penalty_term(0, 1)
-        quantize_slopes(0, 0)
 
-        for i in range(2 * NG):
-            g, a = divmod(i, 2)
-            if i == 1:
-                for f in later[:5]:
+        for g in range(NG):
+            if g == 1:
+                for f in later[:4]:
                     f()
-            if i == 3:
-                for f in later[5:]:
+            if g == 2:
+                for f in later[4:]:
                     f()
-            if g + 1 < NG:
-                turn_joint(g + 1, 2 * a)
-                turn_joint(g + 1, 2 * a + 1)
-            if i == 6:
+            if g == 3:
                 spread_penalty(1)
-            hidden(g, 2 * a)
-            hidden(g, 2 * a + 1)
-            if i in (1, 3, 5):
-                group_slopes(0, (i + 1) // 2, "scalar")
-            if i >= 6:
-                group_slopes(1, i - 6, "scalar")
-            if i == 0:
-                momentum_term(0, 0)
-                momentum_term(0, 1)
-            if g + 1 < NG:
-                quantize_joint(g + 1, a)
-            if g > 0 and a == 0:
-                quantize_h(g - 1)
-            if i == 0:
-                penalty_term(0, 2)
-                penalty_term(0, 3)
-            if i == 1:
-                momentum_term(0, 2)
-                momentum_term(0, 3)
-            if i in (2, 4, 6):
-                quantize_slopes(0, i // 2)
-            weigh(g, 2 * a)
-            weigh(g, 2 * a + 1)
-            if i in (1, 3, 5):
-                group_slopes(0, (i + 1) // 2, "vector")
-            if i >= 6:
-                group_slopes(1, i - 6, "vector")
+            for a in range(2):
+                if g + 1 < NG:
+                    turn_joint(g + 1, 2 * a)
+                    turn_joint(g + 1, 2 * a + 1)
+                hidden(g, 2 * a)
+                hidden(g, 2 * a + 1)
+                if a == 0:
+                    if g == 0:
+                        terms(0, momentum_term)
+                        terms(1, penalty_term)
+                        terms(1, momentum_term)
+                    if g == 2:
+                        group_slopes(1, 0, "vector")
+                    if g == 3:
+                        terms(2, penalty_term)
+                    if g > 0:
+                        group_slopes(0, g, "scalar")
+                        group_slopes(0, g, "vector")
+                        quantize_h(g - 1)
+                    if g == 3:
+                        terms(2, momentum_term)
+                if g == 2 and a == 1:
+                    group_slopes(1, 0, "scalar")
+                if g == 0 and a == 1:
+                    group_slopes(0, 0, "vector")
+                    group_slopes(0, 0, "scalar")
+                if g + 1 < NG:
+                    quantize_joint(g + 1, a)
+            quantize_slopes(0, g)
+            group_slopes(*((0, g + 1) if g + 1 < NG else (1, 1)), "gpsimd")
+            for q in range(4):
+                weigh(g, q)
         load_slopes(2, 0, 2)
         load_slopes(2, 1, 2)
+        load_slopes(2, 2, 2)
         load_state(2, 2)
         load_momentum(2, 2)
-        load_slopes(2, 2, 2)
         load_slopes(2, 3, 2)
+        group_slopes(1, 1, "scalar")
+        group_slopes(1, 2, "scalar")
+        quantize_slopes(1, 0)
         quantize_h(NG - 1)
-        for a in range(NF):
-            for g in range(NG):
-                gradient(0, a, g)
+        group_slopes(1, 2, "vector")
 
-        for c in range(NC - 1):
+        for k in range(2 * NC - 3):
+            c, b = divmod(k, 2)
             n = c + 1
-            group_slopes(n, 2, "scalar")
-            penalty_term(n, 0)
-            penalty_term(n, 1)
-            finish(c, 0)
-            finish(c, 1)
-            round_y(c, 0)
-            round_y(c, 1)
-            turn_y(c, 0)
-            group_slopes(n, 3, "scalar")
-            momentum_term(n, 0)
-            momentum_term(n, 1)
-            group_slopes(n, 3, "vector")
-            if c > 0:
+            for a in (2 * b, 2 * b + 1):
+                for g in range(NG):
+                    gradient(c, a, g)
+            if k > 0:
+                turn_y((k - 1) // 2, (k - 1) % 2)
+            if k == 4:
+                for a in (2, 3):
+                    for g in range(NG):
+                        gradient(c, a, g)
+            if n < NC and k > 0:
+                group_slopes(n, 2 * b + 1, "scalar")
+                group_slopes(n, 2 * b + 1, "vector")
+            if k > 0:
+                group_y((k - 1) // 2, (k - 1) % 2)
+            if n < NC:
+                if k > 0:
+                    quantize_slopes(n, 2 * b)
+                quantize_slopes(n, 2 * b + 1)
+            n2, b2 = divmod(k + 3, 2)
+            if n2 < NC:
+                group_slopes(n2, 2 * b2 + 1, "gpsimd")
+                terms(k + 3, penalty_term)
+            n3, b3 = divmod(k + 4, 2)
+            if n3 < NC:
+                group_slopes(n3, 2 * b3, "scalar")
+            finish(c, 2 * b)
+            finish(c, 2 * b + 1)
+            round_y(c, 2 * b)
+            round_y(c, 2 * b + 1, nc.scalar.copy if k + 1 < 2 * NC else nc.vector.tensor_copy)
+            if n2 < NC and k < 4:
+                terms(k + 3, momentum_term)
+            if n3 < NC:
+                group_slopes(n3, 2 * b3, "vector")
+            if b == 0 and c > 0:
                 quantize_y(c - 1, 0, F)
-            quantize_slopes(n, 0)
-            quantize_slopes(n, 1)
-            for g in range(2):
-                for a in range(2):
-                    gradient(n, a, g)
-            penalty_term(n, 2)
-            penalty_term(n, 3)
-            finish(c, 2)
-            finish(c, 3)
-            group_y(c, 0)
-            round_y(c, 2)
-            round_y(c, 3)
-            for g in range(2):
-                for a in range(2, 4):
-                    gradient(n, a, g)
-            if n + 1 < NC:
-                group_slopes(n + 1, 0, "scalar")
-                group_slopes(n + 1, 1, "scalar")
-            for g in range(2, 4):
-                quantize_slopes(n, g)
-                for a in range(NF):
-                    gradient(n, a, g)
-                if g == 2:
-                    turn_y(c, 1)
-            group_y(c, 1)
-            momentum_term(n, 2)
-            momentum_term(n, 3)
-            if n + 1 < NC:
-                group_slopes(n + 1, 1, "vector")
         c = NC - 1
+        for g in range(2):
+            for a in range(2):
+                gradient(c, a, g)
+        turn_y(c - 1, 0)
+        group_slopes(c, 3, "scalar")
+        group_y(c - 1, 0)
+        finish(c - 1, 2)
+        finish(c - 1, 3)
+        round_y(c - 1, 2)
+        round_y(c - 1, 3)
+        quantize_slopes(c, 2)
+        for g in range(2):
+            for a in range(2, 4):
+                gradient(c, a, g)
+        quantize_slopes(c, 3)
+        for g in range(2, 4):
+            for a in range(NF):
+                gradient(c, a, g)
+        terms(2 * c + 1, momentum_term)
+        turn_y(c - 1, 1)
         for a in range(NF):
             finish(c, a)
-            if a == 1:
-                quantize_y(c - 1, 0, F)
-            if a < 3:
+            if a < 2:
                 round_y(c, a)
-            if a == 1:
-                turn_y(c, 0)
+        group_y(c - 1, 1)
+        turn_y(c, 0)
         group_y(c, 0)
+        round_y(c, 2, nc.vector.tensor_copy)
         round_y(c, 3, nc.vector.tensor_copy)
-        turn_y(c, 1)
+        quantize_y(c - 1, 0, F)
         quantize_y(c, 0, F // 2)
-        group_y(c, 1, nc.vector.tensor_copy)
+        turn_last(c, 2, nc.scalar.copy)
+        turn_last(c, 3, nc.vector.tensor_copy)
         quantize_y(c, F // 2, F)
 
         for q in range(4):
-            nc.sync.dma_start(
+            (nc.sync if q < 2 else nc.scalar).dma_start(
                 out=out_2[:, 4 * q : 4 * q + 4, :].rearrange("g r m -> r g m").bitcast(I32),
                 in_=y_scales[32 * q : 32 * q + 4, :, :].bitcast(I32),
             )

@@ -23,10 +23,23 @@ NG = R // KP
 NS = D // KP
 NC = V // KP
 NF = F // P
-REUSE = [0, 1, 2, 3, 6, 4, 8, 5, 10, 11]
-VEC_COLS = [512,224,224,64, 0,0,0,0, 0,0,96,0, 64,0,0,0]
-W_VEC_COLS = 336
-SIDE_COLS = [0,288,288,448, 0,288,0,288, 0,288,0,288, 0,288,0,288]
+PEN_ROWS = V // (2 * P)
+
+STATE_BANK = 0
+PENALTY_BANKS = (1, 4)
+JOINT_BANKS = (3, 4, 2)
+Y_BANKS = (3, 2)
+HIDDEN_BANKS = (6, 7, 5)
+GRADIENT_BANKS = (5, 6, 7, STATE_BANK)
+
+STAGING_SLOTS = 24
+
+W_VECTOR_COLS = 336
+WINDOW_COLS = 288
+LONG_WINDOW_COLS = 448
+GPSIMD_TILES = [(0, g) for g in range(1, NG)] + [(c, g) for c in range(1, NC) for g in (1, 3)]
+GPSIMD_COLS = {tile: LONG_WINDOW_COLS if tile == (0, NG - 1) else WINDOW_COLS for tile in GPSIMD_TILES}
+VECTOR_COLS = {(0, 0): KP, (0, 1): 64, (0, 2): 64, (2, 2): 64, (3, 0): 64}
 
 
 def tile_transducer_bottleneck_gradient_momen_h3_kernel(
@@ -35,8 +48,7 @@ def tile_transducer_bottleneck_gradient_momen_h3_kernel(
     nc = tc.nc
     with ExitStack() as ctx:
         keep = ctx.enter_context(tc.tile_pool(name="keep", bufs=1))
-        raw = ctx.enter_context(tc.tile_pool(name="raw", bufs=1))
-        wide = ctx.enter_context(tc.tile_pool(name="wide", bufs=1))
+        staging = ctx.enter_context(tc.tile_pool(name="staging", bufs=STAGING_SLOTS))
         work = ctx.enter_context(tc.tile_pool(name="work", bufs=2))
         psum = ctx.enter_context(tc.psum_pool(name="psum", bufs=1))
         ctx.enter_context(tc.manual_schedule())
@@ -49,173 +61,161 @@ def tile_transducer_bottleneck_gradient_momen_h3_kernel(
 
         def interleave(copy, grouped, rows, lo, hi):
             copy(
-                out=grouped[:, PACK * lo : PACK * hi].rearrange("p (c i j) -> p c j i", i=4, j=PACK),
-                in_=rows[:, :, lo:hi].rearrange("p j (c i) -> p c j i", i=4),
+                out=grouped[:, PACK * lo : PACK * hi].rearrange("p (c i t) -> p c t i", i=4, t=PACK),
+                in_=rows[:, :, lo:hi].rearrange("p t (c i) -> p c t i", i=4),
             )
 
         ident = keep.tile([P, P], F32, name="ident")
-        rows = keep.tile([P, KP], BF16, name="rows")
-        row_words = rows[:].bitcast(F32)
-        nc.gpsimd.memset(row_words[0:64, :], 0.0)
+        vectors = keep.tile([P, KP], BF16, name="vectors")
+        vector_words = vectors[:].bitcast(F32)
+        half = P // 2
+        nc.gpsimd.memset(vector_words[0:half, :], 0.0)
         make_identity(nc, ident[:])
         for u in range(2):
             nc.scalar.activation(
-                out=row_words[64:P, u * P : (u + 1) * P], in_=ident[64:P, :], func=ACT.Tanh, scale=0.0
+                out=vector_words[half:P, u * P : (u + 1) * P], in_=ident[half:P, :], func=ACT.Tanh, scale=0.0
             )
 
-        slots = list(range(12)) + REUSE
         j_raw, w_raw, s_raw, b_raw, m_raw = {}, {}, {}, {}, {}
 
-        def load_joint(g, a):
-            j_raw[g, a] = raw.tile([P, 2, D], BF16, name="j_raw", tag="raw%d" % slots.pop(0))
-            src = joint[g * KP : (g + 1) * KP, :].rearrange("(m t) d -> m t d", t=PACK)
-            nc.sync.dma_start(out=j_raw[g, a][:], in_=src[:, 2 * a : 2 * a + 2, :])
+        def load(src):
+            staged = staging.tile(list(src.shape), BF16, name="staged")
+            nc.sync.dma_start(out=staged[:], in_=src)
+            return staged
+
+        def load_joint(g, b):
+            rows = joint[g * KP : (g + 1) * KP, :].rearrange("(m t) d -> m t d", t=PACK)
+            j_raw[g, b] = load(rows[:, 2 * b : 2 * b + 2, :])
 
         def load_w(s):
-            w_raw[s] = raw.tile([P, PACK, F], BF16, name="w_raw", tag="raw%d" % slots.pop(0))
-            src = hidden_w[s * KP : (s + 1) * KP, :].rearrange("(p j) f -> p j f", j=PACK)
-            nc.sync.dma_start(out=w_raw[s][:], in_=src)
+            w_raw[s] = load(hidden_w[s * KP : (s + 1) * KP, :].rearrange("(p t) f -> p t f", t=PACK))
 
-        def load_columns(tiles, key, src, c, n):
-            if n == 1:
-                t = raw.tile([P, 4, KP], BF16, name="narrow", tag="raw%d" % slots.pop(0))
-            else:
-                t = wide.tile([P, 4, n * KP], BF16, name="wide%d" % len(wides))
-                wides.append(t)
-            nc.sync.dma_start(out=t[:], in_=src[:, :, c * KP : (c + n) * KP])
-            for i in range(n):
-                tiles[(c + i,) + key] = t[:, :, i * KP : (i + 1) * KP]
+        def load_slopes(c, g):
+            rows = slopes[g * KP : (g + 1) * KP, c * KP : (c + 1) * KP]
+            s_raw[c, g] = load(rows.rearrange("(p t) v -> p t v", t=PACK))
 
-        wides = []
+        def load_bottleneck(c):
+            b_raw[c] = load(bottleneck[:, c * KP : (c + 1) * KP].rearrange("(a p) v -> p a v", p=P))
 
-        def load_slopes(c, g, n=1):
-            load_columns(s_raw, (g,), slopes[g * KP : (g + 1) * KP, :].rearrange("(p j) v -> p j v", j=PACK), c, n)
+        def load_momentum(c):
+            m_raw[c] = load(momentum[:, c * KP : (c + 1) * KP].rearrange("(a p) v -> p a v", p=P))
 
-        def load_state(c, n=1):
-            load_columns(b_raw, (), bottleneck.rearrange("(a p) v -> p a v", p=P), c, n)
-
-        def load_momentum(c, n=1):
-            load_columns(m_raw, (), momentum.rearrange("(a p) v -> p a v", p=P), c, n)
-
-        load_w(0)
-        load_joint(0, 0)
-        nc.sync.dma_start(out=rows[0:8, 0 : 2 * P], in_=penalty.rearrange("(c w) -> c w", w=2 * P))
-        nc.sync.dma_start(out=rows[8:12, :], in_=state_w.rearrange("(g w) -> g w", w=KP))
-        load_w(1)
-        load_joint(0, 1)
-        load_state(0)
-        load_momentum(0)
-        load_joint(1, 0)
-        load_slopes(0, 0)
-        load_joint(1, 1)
-        load_slopes(0, 1)
-        load_joint(2, 0)
-        load_joint(2, 1)
-        later = [
-            lambda: load_slopes(0, 2),
-            lambda: load_joint(3, 0),
-            lambda: load_joint(3, 1),
-            lambda: load_slopes(0, 3),
-            lambda: load_slopes(1, 0),
-            lambda: load_state(1),
-            lambda: load_slopes(1, 1),
-            lambda: load_momentum(1),
-            lambda: load_slopes(1, 2),
-            lambda: load_slopes(1, 3),
-        ]
-
+        def load_chunk(c):
+            load_slopes(c, 0)
+            load_slopes(c, 1)
+            load_bottleneck(c)
+            load_slopes(c, 2)
+            load_momentum(c)
+            load_slopes(c, 3)
 
         w_codes = keep.tile([P, NS, F], U32, name="w_codes", align_bytes=64)
         w_scales = keep.tile([P, NS, F], U8, name="w_scales", align_bytes=64)
         h_codes = keep.tile([P, NG, F], U32, name="h_codes", align_bytes=64)
         h_scales = keep.tile([P, NG, F], U8, name="h_scales", align_bytes=64)
         y_scales = keep.tile([P, NC, F], U8, name="y_scales", align_bytes=64)
-        pen_cols = keep.tile([P, 8], F32, name="pen_cols")
+        pen_cols = keep.tile([P, PEN_ROWS], F32, name="pen_cols")
         w_grp, j_grp, j_codes, j_scales, tanh_a, h_grp = {}, {}, {}, {}, {}, {}
-        turn = [0, 0]
 
-        def turn_bank():
-            turn[0] += 1
-            return bank(2 + turn[0] % (3 if turn[0] <= 16 else 2), [P, 4, P])
+        def group_w(s):
+            w_grp[s] = work.tile([P, PACK * F], BF16, name="w_grp", tag="grouped", bufs=3, align_bytes=64)
+            interleave(nc.vector.tensor_copy, w_grp[s], w_raw[s][:], 0, W_VECTOR_COLS)
+            interleave(nc.scalar.copy, w_grp[s], w_raw[s][:], W_VECTOR_COLS, F)
 
-        def group_w(s, cut):
-            w_grp[s] = work.tile([P, PACK * F], BF16, name="w_grp", tag="grp", bufs=3, align_bytes=64)
-            interleave(nc.vector.tensor_copy, w_grp[s], w_raw[s][:], 0, cut)
-            if cut < F:
-                interleave(nc.scalar.copy, w_grp[s], w_raw[s][:], cut, F)
+        def quantize_w(s):
+            quantize(w_codes[:, s, :], w_scales[:, s, :], w_grp[s][:])
 
-        def turn_joint(g, t):
-            if t % 2 == 0:
-                j_grp[g, t // 2] = work.tile([P, 2, D], BF16, name="j_grp", bufs=2, align_bytes=64)
-            words = j_raw[g, t // 2][:, t % 2, :].bitcast(F32)
-            turned = turn_bank()
-            for s in range(NS):
-                for u in range(2):
-                    nc.tensor.transpose(turned[:, 2 * s + u, :], words[:, 2 * P * s + u : 2 * P * (s + 1) : 2], ident[:])
-            nc.scalar.copy(
-                out=j_grp[g, t // 2][:, t % 2, :].bitcast(F32).rearrange("p (s r u) -> p s r u", s=NS, u=2),
-                in_=turned[:].rearrange("p (s u) r -> p s r u", u=2),
-            )
-
-        def quantize_joint(g, a):
-            j_codes[g, a] = work.tile([P, 4 * P], U32, name="j_codes", bufs=4, align_bytes=64)
-            j_scales[g, a] = work.tile([P, 4 * P], U8, name="j_scales", bufs=4, align_bytes=64)
-            quantize(j_codes[g, a][:], j_scales[g, a][:], j_grp[g, a][:].rearrange("p t d -> p (t d)"))
-
-        def hidden(g, q):
-            turn[1] += 1
-            acc = bank(5 + turn[1] % 3, [P, PACK, P])
-            cols = slice(q * P, (q + 1) * P)
-            for t in range(PACK):
+        def turn_joint(g, b):
+            j_grp[g, b] = work.tile([P, 2, D], BF16, name="j_grp", align_bytes=64)
+            for i in range(2):
+                words = j_raw[g, b][:, i, :].bitcast(F32)
+                turned = bank(JOINT_BANKS[(PACK * g + 2 * b + i) % len(JOINT_BANKS)], [P, 2 * NS, P])
                 for s in range(NS):
-                    rs = slice((2 * (t % 2) + s) * P, (2 * (t % 2) + s + 1) * P)
-                    nc.tensor.matmul_mx(
-                        out=acc[:, t, :],
-                        lhsT=j_codes[g, t // 2][:, rs].bitcast(FP8X4),
-                        lhsT_scale=j_scales[g, t // 2][:, rs],
-                        rhs=w_codes[:, s, cols].bitcast(FP8X4),
-                        rhs_scale=w_scales[:, s, cols],
-                        start=(s == 0),
-                        stop=(s == NS - 1),
-                    )
-            tanh_a[g, q] = work.tile([P, P, PACK], F32, name="tanh_a", bufs=4)
-            nc.scalar.activation(out=tanh_a[g, q][:], in_=acc[:].rearrange("p t f -> p f t"), func=ACT.Tanh)
+                    for u in range(2):
+                        every_second = words[:, 2 * P * s + u : 2 * P * (s + 1) : 2]
+                        nc.tensor.transpose(turned[:, 2 * s + u, :], every_second, ident[:])
+                nc.scalar.copy(
+                    out=j_grp[g, b][:, i, :].bitcast(F32).rearrange("p (s m u) -> p s m u", s=NS, u=2),
+                    in_=turned[:].rearrange("p (s u) m -> p s m u", u=2),
+                )
 
-        def weigh(g, q):
-            if q == 0:
-                h_grp[g] = work.tile([P, PACK * F], BF16, name="h_grp", bufs=2, align_bytes=64)
-            weights = vec[:].bitcast(BF16)[:, 1:3, 2 * (8 + g) : 2 * (9 + g)]
+        def quantize_joint(g, b):
+            j_codes[g, b] = work.tile([P, 2 * NS * P], U32, name="j_codes", bufs=4, align_bytes=64)
+            j_scales[g, b] = work.tile([P, 2 * NS * P], U8, name="j_scales", bufs=4, align_bytes=64)
+            quantize(j_codes[g, b][:], j_scales[g, b][:], j_grp[g, b][:].rearrange("p i d -> p (i d)"))
+
+        def hidden(g, b):
+            tanh_a[g, b] = work.tile([P, 2, P, PACK], F32, name="tanh_a")
+            for i in range(2):
+                a = 2 * b + i
+                acc = bank(HIDDEN_BANKS[(NF * g + a) % len(HIDDEN_BANKS)], [P, PACK, P])
+                units = slice(a * P, (a + 1) * P)
+                for t in range(PACK):
+                    for s in range(NS):
+                        first = (NS * (t % 2) + s) * P
+                        nc.tensor.matmul_mx(
+                            out=acc[:, t, :],
+                            lhsT=j_codes[g, t // 2][:, first : first + P].bitcast(FP8X4),
+                            lhsT_scale=j_scales[g, t // 2][:, first : first + P],
+                            rhs=w_codes[:, s, units].bitcast(FP8X4),
+                            rhs_scale=w_scales[:, s, units],
+                            start=(s == 0),
+                            stop=(s == NS - 1),
+                        )
+                nc.scalar.activation(
+                    out=tanh_a[g, b][:, i, :, :], in_=acc[:].rearrange("m t f -> m f t"), func=ACT.Tanh
+                )
+
+        def weigh(g, b):
+            if b == 0:
+                h_grp[g] = work.tile([P, PACK * F], BF16, name="h_grp", align_bytes=64)
+            row = PEN_ROWS + g
+            weights = turned_vectors[:].bitcast(BF16)[:, 1:3, 2 * row : 2 * row + 2]
             nc.vector.tensor_tensor(
-                out=h_grp[g][:, q * KP : (q + 1) * KP].rearrange("p (f u e) -> p f u e", u=2, e=2),
-                in0=tanh_a[g, q][:].rearrange("p f (u e) -> p f u e", u=2),
-                in1=weights.rearrange("p u (o e) -> p o u e", o=1).to_broadcast([P, P, 2, 2]),
+                out=h_grp[g][:, 2 * b * KP : 2 * (b + 1) * KP].rearrange("m (f u e) -> m f u e", u=2, e=2),
+                in0=tanh_a[g, b][:].rearrange("m i f (u e) -> m (i f) u e", u=2),
+                in1=weights.rearrange("m u (o e) -> m o u e", o=1).to_broadcast([P, 2 * P, 2, 2]),
                 op=ALU.mult,
             )
 
         def quantize_h(g):
             quantize(h_codes[:, g, :], h_scales[:, g, :], h_grp[g][:])
 
-        s_grp, s_codes, s_scales, pen, prod, rest, g_acc, y, y_bf, y_turned, y_grp = ({} for i in range(11))
+        s_grp, s_codes, s_scales, pen, prod, rest = {}, {}, {}, {}, {}, {}
+        g_acc, y, y_bf, y_turned, y_grp, y_codes = {}, {}, {}, {}, {}, {}
 
-        def group_slopes(c, g, part):
-            side = c == 0 or g % 2 == 1
+        def slopes_share(c, g):
             if (c, g) not in s_grp:
+                single = (c, g) in GPSIMD_COLS or (c, g) == (0, 0)
                 s_grp[c, g] = work.tile(
-                    [P, PACK * KP], BF16, name="s_grp", tag="side" if side else "grp", bufs=1 if side else 3, align_bytes=64
+                    [P, PACK * KP],
+                    BF16,
+                    name="s_grp",
+                    tag="single" if single else "grouped",
+                    bufs=1 if single else 3,
+                    align_bytes=64,
                 )
-            src = s_raw[c, g]
-            lo = SIDE_COLS[4 * c + g]
-            hi = lo + VEC_COLS[4 * c + g]
-            if part == "scalar" and hi < KP:
-                interleave(nc.scalar.copy, s_grp[c, g], src, hi, KP)
-            if part == "vector" and hi > lo:
-                interleave(nc.vector.tensor_copy, s_grp[c, g], src, lo, hi)
-            if part == "gpsimd" and lo > 0:
-                nc.gpsimd.tensor_scalar(
-                    out=s_grp[c, g][:, 0 : PACK * lo].rearrange("p (v j) -> p v j", j=PACK),
-                    in0=src[:, :, 0:lo].rearrange("p j v -> p v j"),
-                    scalar1=1.0, scalar2=0.0, op0=ALU.mult, op1=ALU.add,
-                )
+            lo = GPSIMD_COLS.get((c, g), 0)
+            return s_grp[c, g], lo, lo + VECTOR_COLS.get((c, g), 0)
+
+        def group_on_gpsimd(c, g):
+            grouped, lo, hi = slopes_share(c, g)
+            nc.gpsimd.tensor_scalar(
+                out=grouped[:, 0 : PACK * lo].rearrange("p (v t) -> p v t", t=PACK),
+                in0=s_raw[c, g][:, :, 0:lo].rearrange("p t v -> p v t"),
+                scalar1=1.0,
+                scalar2=0.0,
+                op0=ALU.mult,
+                op1=ALU.add,
+            )
+
+        def group_on_vector(c, g):
+            grouped, lo, hi = slopes_share(c, g)
+            if hi > lo:
+                interleave(nc.vector.tensor_copy, grouped, s_raw[c, g][:], lo, hi)
+
+        def group_on_scalar(c, g):
+            grouped, lo, hi = slopes_share(c, g)
+            interleave(nc.scalar.copy, grouped, s_raw[c, g][:], hi, KP)
 
         def quantize_slopes(c, g):
             if g == 0:
@@ -224,235 +224,246 @@ def tile_transducer_bottleneck_gradient_momen_h3_kernel(
             quantize(s_codes[c][:, g, :], s_scales[c][:, g, :], s_grp[c, g][:])
 
         def spread_penalty(h):
-            pen[h] = bank((1, 4)[h], [P, 4, P])
+            pen[h] = bank(PENALTY_BANKS[h], [P, 4, P])
             for i in range(4):
-                col = pen_cols[:, 4 * h + i : 4 * h + i + 1]
-                nc.tensor.transpose(pen[h][:, i, :], col.to_broadcast([P, P]), ident[:])
+                column = pen_cols[:, 4 * h + i : 4 * h + i + 1]
+                nc.tensor.transpose(pen[h][:, i, :], column.to_broadcast([P, P]), ident[:])
 
-        def penalty_term(c, a):
-            cols = slice((c % 2) * KP, (c % 2 + 1) * KP)
-            prod[c, a] = work.tile([P, KP], F32, name="prod", bufs=2)
+        def penalty_term(j):
+            c, b = divmod(j, 2)
+            row = pen[c // 2][:].rearrange("p i w -> p (i w)").bitcast(BF16)[:, (c % 2) * KP : (c % 2 + 1) * KP]
+            prod[j] = work.tile([P, 2, KP], F32, name="prod")
             nc.vector.tensor_tensor(
-                out=prod[c, a][:],
-                in0=b_raw[c,][:, a, :],
-                in1=pen[c // 2][:].rearrange("p i w -> p (i w)").bitcast(BF16)[:, cols],
+                out=prod[j][:],
+                in0=b_raw[c][:, 2 * b : 2 * b + 2, :],
+                in1=row.rearrange("p (o v) -> p o v", o=1).to_broadcast([P, 2, KP]),
                 op=ALU.mult,
             )
 
-        def momentum_term(c, a):
-            cols = slice((c % 2) * KP, (c % 2 + 1) * KP)
-            rest[c, a] = work.tile([P, KP], F32, name="rest", bufs=8)
+        def momentum_term(j):
+            c, b = divmod(j, 2)
+            rest[j] = work.tile([P, 2, KP], F32, name="rest", bufs=4)
             nc.vector.scalar_tensor_tensor(
-                out=rest[c, a][:], in0=m_raw[c,][:, a, :], scalar=BETA, in1=prod[c, a][:],
-                op0=ALU.mult, op1=ALU.add,
+                out=rest[j][:],
+                in0=m_raw[c][:, 2 * b : 2 * b + 2, :],
+                scalar=BETA,
+                in1=prod[j][:],
+                op0=ALU.mult,
+                op1=ALU.add,
             )
 
         def gradient(c, a, g):
             if g == 0:
-                g_acc[c, a] = bank((5, 6, 7, 0)[a], [P, KP])
-            cols = slice(a * P, (a + 1) * P)
+                g_acc[c, a] = bank(GRADIENT_BANKS[a], [P, KP])
+            units = slice(a * P, (a + 1) * P)
             nc.tensor.matmul_mx(
                 out=g_acc[c, a][:],
-                lhsT=h_codes[:, g, cols].bitcast(FP8X4),
-                lhsT_scale=h_scales[:, g, cols],
+                lhsT=h_codes[:, g, units].bitcast(FP8X4),
+                lhsT_scale=h_scales[:, g, units],
                 rhs=s_codes[c][:, g, :].bitcast(FP8X4),
                 rhs_scale=s_scales[c][:, g, :],
                 start=(g == 0),
                 stop=(g == NG - 1),
             )
 
+        def gradient_pair(j):
+            c, b = divmod(j, 2)
+            for a in (2 * b, 2 * b + 1):
+                for g in range(NG):
+                    gradient(c, a, g)
+
         def finish(c, a):
             y[c, a] = work.tile([P, KP], F32, name="y", bufs=6)
-            nc.vector.tensor_tensor(out=y[c, a][:], in0=g_acc[c, a][:], in1=rest[c, a][:], op=ALU.add)
+            nc.vector.tensor_tensor(
+                out=y[c, a][:], in0=g_acc[c, a][:], in1=rest[2 * c + a // 2][:, a % 2, :], op=ALU.add
+            )
             nc.sync.dma_start(out=out_0[a * P : (a + 1) * P, c * KP : (c + 1) * KP], in_=y[c, a][:])
 
         def round_y(c, a, copy=nc.scalar.copy):
             y_bf[c, a] = work.tile([P, 2, P, 2], BF16, name="y_bf", bufs=4)
             copy(out=y_bf[c, a][:], in_=y[c, a][:].rearrange("f (p u e) -> f u p e", u=2, e=2))
 
-        def turn_y(c, b):
-            turned = y_turned[c, b] = turn_bank()
-            for a in range(2):
-                words = y_bf[c, 2 * b + a][:].rearrange("f u p e -> f (u p e)").bitcast(F32)
-                for u in range(2):
-                    nc.tensor.transpose(turned[:, 2 * a + u, :], words[:, u * P : (u + 1) * P], ident[:])
-
-        def group_y(c, b, copy=nc.scalar.copy):
-            if b == 0:
-                y_grp[c] = work.tile([P, PACK * F], BF16, name="y_grp", align_bytes=64)
-            copy(
-                out=y_grp[c][:].bitcast(F32)[:, b * KP : (b + 1) * KP].rearrange("p (a f u) -> p a f u", a=2, u=2),
-                in_=y_turned[c, b][:].rearrange("p (a u) f -> p a f u", u=2),
-            )
-
-        def turn_last(c, a, copy):
-            turned = bank(2 + a % 2, [P, 2, P])
+        def turn_y_tile(c, a, turned):
             words = y_bf[c, a][:].rearrange("f u p e -> f (u p e)").bitcast(F32)
             for u in range(2):
                 nc.tensor.transpose(turned[:, u, :], words[:, u * P : (u + 1) * P], ident[:])
+
+        def turn_y(j):
+            c, b = divmod(j, 2)
+            y_turned[j] = bank(Y_BANKS[j % 2], [P, 4, P])
+            for i in range(2):
+                turn_y_tile(c, 2 * b + i, y_turned[j][:, 2 * i : 2 * i + 2, :])
+
+        def group_y(j):
+            c, b = divmod(j, 2)
+            if b == 0:
+                y_grp[c] = work.tile([P, PACK * F], BF16, name="y_grp", align_bytes=64)
+            nc.scalar.copy(
+                out=y_grp[c][:].bitcast(F32)[:, b * KP : (b + 1) * KP].rearrange("p (i f u) -> p i f u", i=2, u=2),
+                in_=y_turned[j][:].rearrange("p (i u) f -> p i f u", u=2),
+            )
+
+        def turn_and_group_tile(c, a, copy):
+            turned = bank(Y_BANKS[(a + 1) % 2], [P, 2, P])
+            turn_y_tile(c, a, turned[:])
             copy(
                 out=y_grp[c][:].bitcast(F32)[:, a * 2 * P : (a + 1) * 2 * P].rearrange("p (f u) -> p f u", u=2),
                 in_=turned[:].rearrange("p u f -> p f u"),
             )
 
         def quantize_y(c, lo, hi):
-            y_codes = work.tile([P, F], U32, name="y_codes", bufs=3, align_bytes=64)
-            quantize(y_codes[:, lo:hi], y_scales[:, c, lo:hi], y_grp[c][:, PACK * lo : PACK * hi])
-            dst = out_1[c, :, :, :].rearrange("p m t -> p (m t)").bitcast(I32)
-            nc.sync.dma_start(out=dst[:, lo:hi], in_=y_codes[:, lo:hi].bitcast(I32))
+            if lo == 0:
+                y_codes[c] = work.tile([P, F], U32, name="y_codes", align_bytes=64)
+            quantize(y_codes[c][:, lo:hi], y_scales[:, c, lo:hi], y_grp[c][:, PACK * lo : PACK * hi])
+            words = out_1[c, :, :, :].rearrange("p f t -> p (f t)").bitcast(I32)
+            nc.sync.dma_start(out=words[:, lo:hi], in_=y_codes[c][:, lo:hi].bitcast(I32))
 
-        def terms(j, which):
-            c, b = divmod(j, 2)
-            for a in (2 * b, 2 * b + 1):
-                which(c, a)
+        load_w(0)
+        load_joint(0, 0)
+        nc.sync.dma_start(out=vectors[0:PEN_ROWS, 0 : 2 * P], in_=penalty.rearrange("(i w) -> i w", w=2 * P))
+        nc.sync.dma_start(out=vectors[PEN_ROWS : PEN_ROWS + NG, :], in_=state_w.rearrange("(g r) -> g r", r=KP))
+        load_w(1)
+        load_joint(0, 1)
+        load_bottleneck(0)
+        load_joint(1, 0)
+        load_momentum(0)
+        load_joint(1, 1)
+        load_slopes(0, 0)
+        load_joint(2, 0)
+        load_slopes(0, 1)
+        load_joint(2, 1)
+        load_slopes(0, 2)
+        load_joint(3, 0)
+        load_joint(3, 1)
+        load_slopes(0, 3)
+        load_chunk(1)
 
-        group_w(0, W_VEC_COLS)
+        group_w(0)
         turn_joint(0, 0)
-        turn_joint(0, 1)
-        vec = bank(0, [P, 3, P])
-        nc.tensor.transpose(vec[:, 0, :], row_words[:, 0:P], ident[:])
+        turned_vectors = bank(STATE_BANK, [P, 3, P])
+        nc.tensor.transpose(turned_vectors[:, 0, :], vector_words[:, 0:P], ident[:])
         for u in range(2):
-            nc.tensor.transpose(vec[:, 1 + u, :], row_words[:, u : 2 * P : 2], ident[:])
-        nc.scalar.copy(out=pen_cols[:], in_=vec[:, 0, 0:8])
-        quantize(w_codes[:, 0, :], w_scales[:, 0, :], w_grp[0][:])
-        group_w(1, W_VEC_COLS)
+            nc.tensor.transpose(turned_vectors[:, 1 + u, :], vector_words[:, u : 2 * P : 2], ident[:])
+        nc.scalar.copy(out=pen_cols[:], in_=turned_vectors[:, 0, 0:PEN_ROWS])
+        quantize_w(0)
+        group_w(1)
         quantize_joint(0, 0)
         spread_penalty(0)
-        turn_joint(0, 2)
-        turn_joint(0, 3)
-        quantize(w_codes[:, 1, :], w_scales[:, 1, :], w_grp[1][:])
-        terms(0, penalty_term)
+        turn_joint(0, 1)
+        quantize_w(1)
+        penalty_term(0)
         quantize_joint(0, 1)
 
+        last_g = NG - 1
         for g in range(NG):
-            if g == 1:
-                for f in later[:4]:
-                    f()
-            if g == 2:
-                for f in later[4:]:
-                    f()
-            if g == 3:
+            if g < last_g:
+                turn_joint(g + 1, 0)
+            else:
                 spread_penalty(1)
-            for a in range(2):
-                if g + 1 < NG:
-                    turn_joint(g + 1, 2 * a)
-                    turn_joint(g + 1, 2 * a + 1)
-                hidden(g, 2 * a)
-                hidden(g, 2 * a + 1)
-                if a == 0:
-                    if g == 0:
-                        terms(0, momentum_term)
-                        terms(1, penalty_term)
-                        terms(1, momentum_term)
-                    if g == 2:
-                        group_slopes(1, 0, "vector")
-                    if g == 3:
-                        terms(2, penalty_term)
-                    if g > 0:
-                        group_slopes(0, g, "scalar")
-                        group_slopes(0, g, "vector")
-                        quantize_h(g - 1)
-                    if g == 3:
-                        terms(2, momentum_term)
-                if g == 2 and a == 1:
-                    group_slopes(1, 0, "scalar")
-                if g == 0 and a == 1:
-                    group_slopes(0, 0, "vector")
-                    group_slopes(0, 0, "scalar")
-                if g + 1 < NG:
-                    quantize_joint(g + 1, a)
+            if g > 0:
+                group_on_scalar(0, g)
+            hidden(g, 0)
+            if g == 0:
+                penalty_term(1)
+                momentum_term(0)
+            else:
+                if g == last_g:
+                    penalty_term(2)
+                group_on_vector(0, g)
+                quantize_h(g - 1)
+            if g < last_g:
+                quantize_joint(g + 1, 0)
+                turn_joint(g + 1, 1)
+            else:
+                momentum_term(2)
+            hidden(g, 1)
+            if g == 0:
+                momentum_term(1)
+                group_on_vector(0, 0)
+            if g == last_g - 1:
+                group_on_scalar(1, 0)
+            if g < last_g:
+                quantize_joint(g + 1, 1)
             quantize_slopes(0, g)
-            group_slopes(*((0, g + 1) if g + 1 < NG else (1, 1)), "gpsimd")
-            for q in range(4):
-                weigh(g, q)
-        load_slopes(2, 0, 2)
-        load_slopes(2, 1, 2)
-        load_slopes(2, 2, 2)
-        load_state(2, 2)
-        load_momentum(2, 2)
-        load_slopes(2, 3, 2)
-        group_slopes(1, 1, "scalar")
-        group_slopes(1, 2, "scalar")
+            if g < last_g:
+                group_on_gpsimd(0, g + 1)
+            else:
+                group_on_gpsimd(1, 1)
+            weigh(g, 0)
+            weigh(g, 1)
+        load_chunk(2)
+        load_chunk(3)
+        group_on_scalar(1, 1)
+        group_on_scalar(1, 2)
         quantize_slopes(1, 0)
-        quantize_h(NG - 1)
-        group_slopes(1, 2, "vector")
+        quantize_h(last_g)
 
-        for k in range(2 * NC - 3):
-            c, b = divmod(k, 2)
-            n = c + 1
-            for a in (2 * b, 2 * b + 1):
-                for g in range(NG):
-                    gradient(c, a, g)
-            if k > 0:
-                turn_y((k - 1) // 2, (k - 1) % 2)
-            if k == 4:
-                for a in (2, 3):
-                    for g in range(NG):
-                        gradient(c, a, g)
-            if n < NC and k > 0:
-                group_slopes(n, 2 * b + 1, "scalar")
-                group_slopes(n, 2 * b + 1, "vector")
-            if k > 0:
-                group_y((k - 1) // 2, (k - 1) % 2)
-            if n < NC:
-                if k > 0:
-                    quantize_slopes(n, 2 * b)
-                quantize_slopes(n, 2 * b + 1)
-            n2, b2 = divmod(k + 3, 2)
-            if n2 < NC:
-                group_slopes(n2, 2 * b2 + 1, "gpsimd")
-                terms(k + 3, penalty_term)
-            n3, b3 = divmod(k + 4, 2)
-            if n3 < NC:
-                group_slopes(n3, 2 * b3, "scalar")
+        last_full = 2 * NC - 4
+        for j in range(last_full + 1):
+            c, b = divmod(j, 2)
+            gradient_pair(j)
+            if j > 0:
+                turn_y(j - 1)
+            if j == last_full:
+                gradient_pair(j + 1)
+            if j > 0:
+                group_on_scalar(c + 1, 2 * b + 1)
+                group_y(j - 1)
+                quantize_slopes(c + 1, 2 * b)
+            quantize_slopes(c + 1, 2 * b + 1)
+            group_on_gpsimd((j + 3) // 2, 2 * ((j + 3) % 2) + 1)
+            penalty_term(j + 3)
+            if j < last_full:
+                group_on_scalar(c + 2, 2 * b)
             finish(c, 2 * b)
             finish(c, 2 * b + 1)
             round_y(c, 2 * b)
-            round_y(c, 2 * b + 1, nc.scalar.copy if k + 1 < 2 * NC else nc.vector.tensor_copy)
-            if n2 < NC and k < 4:
-                terms(k + 3, momentum_term)
-            if n3 < NC:
-                group_slopes(n3, 2 * b3, "vector")
+            round_y(c, 2 * b + 1)
+            if j < last_full:
+                momentum_term(j + 3)
+                group_on_vector(c + 2, 2 * b)
             if b == 0 and c > 0:
                 quantize_y(c - 1, 0, F)
+
         c = NC - 1
         for g in range(2):
             for a in range(2):
                 gradient(c, a, g)
-        turn_y(c - 1, 0)
-        group_slopes(c, 3, "scalar")
-        group_y(c - 1, 0)
-        finish(c - 1, 2)
-        finish(c - 1, 3)
-        round_y(c - 1, 2)
-        round_y(c - 1, 3)
+        turn_y(last_full)
+        group_on_scalar(c, 3)
+        group_y(last_full)
+        for a in (2, 3):
+            finish(c - 1, a)
+        for a in (2, 3):
+            round_y(c - 1, a)
         quantize_slopes(c, 2)
         for g in range(2):
-            for a in range(2, 4):
+            for a in (2, 3):
                 gradient(c, a, g)
         quantize_slopes(c, 3)
-        for g in range(2, 4):
+        for g in (2, 3):
             for a in range(NF):
                 gradient(c, a, g)
-        terms(2 * c + 1, momentum_term)
-        turn_y(c - 1, 1)
+        momentum_term(2 * c + 1)
+        turn_y(2 * c - 1)
         for a in range(NF):
             finish(c, a)
             if a < 2:
                 round_y(c, a)
-        group_y(c - 1, 1)
-        turn_y(c, 0)
-        group_y(c, 0)
-        round_y(c, 2, nc.vector.tensor_copy)
-        round_y(c, 3, nc.vector.tensor_copy)
+        group_y(2 * c - 1)
+        turn_y(2 * c)
+        group_y(2 * c)
+        for a in (2, 3):
+            round_y(c, a, nc.vector.tensor_copy)
         quantize_y(c - 1, 0, F)
         quantize_y(c, 0, F // 2)
-        turn_last(c, 2, nc.scalar.copy)
-        turn_last(c, 3, nc.vector.tensor_copy)
+        turn_and_group_tile(c, 2, nc.scalar.copy)
+        turn_and_group_tile(c, 3, nc.vector.tensor_copy)
         quantize_y(c, F // 2, F)
 
         for q in range(4):
-            (nc.sync if q < 2 else nc.scalar).dma_start(
-                out=out_2[:, 4 * q : 4 * q + 4, :].rearrange("g r m -> r g m").bitcast(I32),
+            queue = nc.sync if q < 2 else nc.scalar
+            queue.dma_start(
+                out=out_2[:, 4 * q : 4 * q + 4, :].rearrange("c r f -> r c f").bitcast(I32),
                 in_=y_scales[32 * q : 32 * q + 4, :, :].bitcast(I32),
             )

@@ -31,15 +31,18 @@ JOINT_BANKS = (3, 4, 2)
 Y_BANKS = (3, 2)
 HIDDEN_BANKS = (6, 7, 5)
 GRADIENT_BANKS = (5, 6, 7, STATE_BANK)
+LAST_BANKS = PENALTY_BANKS + GRADIENT_BANKS[:2]
 
-STAGING_SLOTS = 24
+STAGING_SLOTS = 16
+
+TERMS = (0, 2, 1, 3, 4, 6, 5, 7)
 
 W_VECTOR_COLS = 336
-WINDOW_COLS = 288
-LONG_WINDOW_COLS = 448
+WINDOW_COLS = 272
+LONG_WINDOW_COLS = 432
 GPSIMD_TILES = [(0, g) for g in range(1, NG)] + [(c, g) for c in range(1, NC) for g in (1, 3)]
 GPSIMD_COLS = {tile: LONG_WINDOW_COLS if tile == (0, NG - 1) else WINDOW_COLS for tile in GPSIMD_TILES}
-VECTOR_COLS = {(0, 0): KP, (0, 1): 64, (0, 2): 64, (2, 2): 64, (3, 0): 64}
+VECTOR_COLS = {(0, 0): KP, (0, 1): 80, (0, 2): 80, (2, 0): 48, (2, 2): 48}
 
 
 def tile_transducer_bottleneck_gradient_momen_h3_kernel(
@@ -92,21 +95,21 @@ def tile_transducer_bottleneck_gradient_momen_h3_kernel(
 
         def load_slopes(c, g):
             rows = slopes[g * KP : (g + 1) * KP, c * KP : (c + 1) * KP]
-            s_raw[c, g] = load(rows.rearrange("(p t) v -> p t v", t=PACK))
+            s_raw[c, g] = load(rows.rearrange("(p t) v -> p t v", t=PACK))[:]
 
-        def load_bottleneck(c):
-            b_raw[c] = load(bottleneck[:, c * KP : (c + 1) * KP].rearrange("(a p) v -> p a v", p=P))
+        def load_slopes_twice_as_wide(c, g):
+            rows = slopes[g * KP : (g + 1) * KP, c * KP : (c + 2) * KP]
+            staged = keep.tile([P, PACK, 2 * KP], BF16, name="wide%d" % g)
+            nc.sync.dma_start(out=staged[:], in_=rows.rearrange("(p t) v -> p t v", t=PACK))
+            for i in range(2):
+                s_raw[c + i, g] = staged[:, :, i * KP : (i + 1) * KP]
 
-        def load_momentum(c):
-            m_raw[c] = load(momentum[:, c * KP : (c + 1) * KP].rearrange("(a p) v -> p a v", p=P))
-
-        def load_chunk(c):
-            load_slopes(c, 0)
-            load_slopes(c, 1)
-            load_bottleneck(c)
-            load_slopes(c, 2)
-            load_momentum(c)
-            load_slopes(c, 3)
+        def load_pairs(tiles, src, j):
+            c, b = divmod(j, 2)
+            rows = src[2 * b * P : 2 * (b + 1) * P, c * KP : (c + 2) * KP]
+            staged = load(rows.rearrange("(i p) v -> p i v", p=P))
+            tiles[j] = staged[:, :, 0:KP]
+            tiles[j + 2] = staged[:, :, KP : 2 * KP]
 
         w_codes = keep.tile([P, NS, F], U32, name="w_codes", align_bytes=64)
         w_scales = keep.tile([P, NS, F], U8, name="w_scales", align_bytes=64)
@@ -211,11 +214,11 @@ def tile_transducer_bottleneck_gradient_momen_h3_kernel(
         def group_on_vector(c, g):
             grouped, lo, hi = slopes_share(c, g)
             if hi > lo:
-                interleave(nc.vector.tensor_copy, grouped, s_raw[c, g][:], lo, hi)
+                interleave(nc.vector.tensor_copy, grouped, s_raw[c, g], lo, hi)
 
         def group_on_scalar(c, g):
             grouped, lo, hi = slopes_share(c, g)
-            interleave(nc.scalar.copy, grouped, s_raw[c, g][:], hi, KP)
+            interleave(nc.scalar.copy, grouped, s_raw[c, g], hi, KP)
 
         def quantize_slopes(c, g):
             if g == 0:
@@ -235,7 +238,7 @@ def tile_transducer_bottleneck_gradient_momen_h3_kernel(
             prod[j] = work.tile([P, 2, KP], F32, name="prod")
             nc.vector.tensor_tensor(
                 out=prod[j][:],
-                in0=b_raw[c][:, 2 * b : 2 * b + 2, :],
+                in0=b_raw[j],
                 in1=row.rearrange("p (o v) -> p o v", o=1).to_broadcast([P, 2, KP]),
                 op=ALU.mult,
             )
@@ -245,7 +248,7 @@ def tile_transducer_bottleneck_gradient_momen_h3_kernel(
             rest[j] = work.tile([P, 2, KP], F32, name="rest", bufs=4)
             nc.vector.scalar_tensor_tensor(
                 out=rest[j][:],
-                in0=m_raw[c][:, 2 * b : 2 * b + 2, :],
+                in0=m_raw[j],
                 scalar=BETA,
                 in1=prod[j][:],
                 op0=ALU.mult,
@@ -254,7 +257,7 @@ def tile_transducer_bottleneck_gradient_momen_h3_kernel(
 
         def gradient(c, a, g):
             if g == 0:
-                g_acc[c, a] = bank(GRADIENT_BANKS[a], [P, KP])
+                g_acc[c, a] = bank((GRADIENT_BANKS if c < NC - 1 else LAST_BANKS)[a], [P, KP])
             units = slice(a * P, (a + 1) * P)
             nc.tensor.matmul_mx(
                 out=g_acc[c, a][:],
@@ -324,9 +327,9 @@ def tile_transducer_bottleneck_gradient_momen_h3_kernel(
         nc.sync.dma_start(out=vectors[PEN_ROWS : PEN_ROWS + NG, :], in_=state_w.rearrange("(g r) -> g r", r=KP))
         load_w(1)
         load_joint(0, 1)
-        load_bottleneck(0)
+        load_pairs(b_raw, bottleneck, 0)
         load_joint(1, 0)
-        load_momentum(0)
+        load_pairs(m_raw, momentum, 0)
         load_joint(1, 1)
         load_slopes(0, 0)
         load_joint(2, 0)
@@ -336,7 +339,6 @@ def tile_transducer_bottleneck_gradient_momen_h3_kernel(
         load_joint(3, 0)
         load_joint(3, 1)
         load_slopes(0, 3)
-        load_chunk(1)
 
         group_w(0)
         turn_joint(0, 0)
@@ -351,7 +353,7 @@ def tile_transducer_bottleneck_gradient_momen_h3_kernel(
         spread_penalty(0)
         turn_joint(0, 1)
         quantize_w(1)
-        penalty_term(0)
+        penalty_term(TERMS[0])
         quantize_joint(0, 1)
 
         last_g = NG - 1
@@ -360,25 +362,32 @@ def tile_transducer_bottleneck_gradient_momen_h3_kernel(
                 turn_joint(g + 1, 0)
             else:
                 spread_penalty(1)
+            if g == 1:
+                load_slopes(1, 0)
+                load_slopes(1, 1)
+                load_pairs(b_raw, bottleneck, 1)
+                load_slopes(1, 2)
+                load_pairs(m_raw, momentum, 1)
+                load_slopes(1, 3)
             if g > 0:
                 group_on_scalar(0, g)
             hidden(g, 0)
             if g == 0:
-                penalty_term(1)
-                momentum_term(0)
+                penalty_term(TERMS[1])
+                momentum_term(TERMS[0])
             else:
                 if g == last_g:
-                    penalty_term(2)
+                    penalty_term(TERMS[2])
                 group_on_vector(0, g)
                 quantize_h(g - 1)
             if g < last_g:
                 quantize_joint(g + 1, 0)
                 turn_joint(g + 1, 1)
             else:
-                momentum_term(2)
+                momentum_term(TERMS[2])
             hidden(g, 1)
             if g == 0:
-                momentum_term(1)
+                momentum_term(TERMS[1])
                 group_on_vector(0, 0)
             if g == last_g - 1:
                 group_on_scalar(1, 0)
@@ -391,60 +400,66 @@ def tile_transducer_bottleneck_gradient_momen_h3_kernel(
                 group_on_gpsimd(1, 1)
             weigh(g, 0)
             weigh(g, 1)
-        load_chunk(2)
-        load_chunk(3)
+        load_slopes_twice_as_wide(2, 0)
+        load_slopes_twice_as_wide(2, 1)
+        load_pairs(b_raw, bottleneck, 4)
+        load_slopes_twice_as_wide(2, 2)
+        load_pairs(m_raw, momentum, 4)
+        load_slopes_twice_as_wide(2, 3)
         group_on_scalar(1, 1)
         group_on_scalar(1, 2)
         quantize_slopes(1, 0)
         quantize_h(last_g)
+        gradient_pair(0)
 
         last_full = 2 * NC - 4
         for j in range(last_full + 1):
             c, b = divmod(j, 2)
-            gradient_pair(j)
+            if j > 0:
+                quantize_slopes(c + 1, 2 * b)
+                momentum_term(TERMS[j + 2])
+            quantize_slopes(c + 1, 2 * b + 1)
+            gradient_pair(j + 1)
             if j > 0:
                 turn_y(j - 1)
-            if j == last_full:
-                gradient_pair(j + 1)
-            if j > 0:
-                group_on_scalar(c + 1, 2 * b + 1)
-                group_y(j - 1)
-                quantize_slopes(c + 1, 2 * b)
-            quantize_slopes(c + 1, 2 * b + 1)
-            group_on_gpsimd((j + 3) // 2, 2 * ((j + 3) % 2) + 1)
-            penalty_term(j + 3)
+            shared = ((j + 3) // 2, 2 * ((j + 3) % 2) + 1)
+            group_on_gpsimd(*shared)
+            group_on_scalar(*shared)
+            penalty_term(TERMS[j + 3])
             if j < last_full:
                 group_on_scalar(c + 2, 2 * b)
+            if j > 0:
+                group_y(j - 1)
             finish(c, 2 * b)
             finish(c, 2 * b + 1)
+            if j == 0:
+                load_pairs(b_raw, bottleneck, 5)
+                load_pairs(m_raw, momentum, 5)
             round_y(c, 2 * b)
             round_y(c, 2 * b + 1)
             if j < last_full:
-                momentum_term(j + 3)
                 group_on_vector(c + 2, 2 * b)
-            if b == 0 and c > 0:
+            if b == 1 and c > 0:
                 quantize_y(c - 1, 0, F)
 
         c = NC - 1
-        for g in range(2):
-            for a in range(2):
+        for a in range(NF):
+            for g in range(2):
                 gradient(c, a, g)
-        turn_y(last_full)
-        group_on_scalar(c, 3)
-        group_y(last_full)
+        quantize_slopes(c, 2)
+        quantize_slopes(c, 3)
+        for a in range(NF):
+            gradient(c, a, 2)
+        turn_y(2 * c - 2)
+        for a in range(NF):
+            gradient(c, a, 3)
         for a in (2, 3):
             finish(c - 1, a)
         for a in (2, 3):
             round_y(c - 1, a)
-        quantize_slopes(c, 2)
-        for g in range(2):
-            for a in (2, 3):
-                gradient(c, a, g)
-        quantize_slopes(c, 3)
-        for g in (2, 3):
-            for a in range(NF):
-                gradient(c, a, g)
-        momentum_term(2 * c + 1)
+        group_y(2 * c - 2)
+        momentum_term(TERMS[-1])
+        quantize_y(c - 2, 0, F)
         turn_y(2 * c - 1)
         for a in range(NF):
             finish(c, a)

from contextlib import ExitStack

import concourse.mybir as mybir
from concourse.masks import make_identity

R, D, F, V = 2048, 1024, 512, 2048
BETA = 0.9
FLOPS = 2 * R * D * F + 2 * R * F * V

F32 = mybir.dt.float32
BF16 = mybir.dt.bfloat16
U32 = mybir.dt.uint32
I32 = mybir.dt.int32
U8 = mybir.dt.uint8
FP8X4 = mybir.dt.float8_e4m3fn_x4
ALU = mybir.AluOpType
ACT = mybir.ActivationFunctionType

P = 128
PACK = 4
KP = P * PACK
NG = R // KP
NS = D // KP
NC = V // KP
NF = F // P
PEN_ROWS = V // (2 * P)

STATE_BANK = 0
PENALTY_BANKS = (1, 4)
JOINT_BANKS = (3, 4, 2)
Y_BANKS = (3, 2)
HIDDEN_BANKS = (6, 7, 5)
GRADIENT_BANKS = (5, 6, 7, STATE_BANK)
LAST_BANKS = PENALTY_BANKS + GRADIENT_BANKS[:2]

STAGING_SLOTS = 16

TERMS = (0, 2, 1, 3, 4, 6, 5, 7)

W_VECTOR_COLS = 336
WINDOW_COLS = 272
LONG_WINDOW_COLS = 432
GPSIMD_TILES = [(0, g) for g in range(1, NG)] + [(c, g) for c in range(1, NC) for g in (1, 3)]
GPSIMD_COLS = {tile: LONG_WINDOW_COLS if tile == (0, NG - 1) else WINDOW_COLS for tile in GPSIMD_TILES}
VECTOR_COLS = {(0, 0): KP, (0, 1): 80, (0, 2): 80, (2, 0): 48, (2, 2): 48}


def tile_transducer_bottleneck_gradient_momen_h3_kernel(
    tc, joint, hidden_w, state_w, slopes, bottleneck, penalty, momentum, out_0, out_1, out_2
):
    nc = tc.nc
    with ExitStack() as ctx:
        keep = ctx.enter_context(tc.tile_pool(name="keep", bufs=1))
        staging = ctx.enter_context(tc.tile_pool(name="staging", bufs=STAGING_SLOTS))
        work = ctx.enter_context(tc.tile_pool(name="work", bufs=2))
        psum = ctx.enter_context(tc.psum_pool(name="psum", bufs=1))
        ctx.enter_context(tc.manual_schedule())

        def bank(i, shape):
            return psum.tile(shape, F32, name="bank", tag="bank%d" % i)

        def quantize(codes, scales, grouped):
            nc.vector.quantize_mx(out=codes.bitcast(FP8X4), scales=scales, in_=grouped)

        def interleave(copy, grouped, rows, lo, hi):
            copy(
                out=grouped[:, PACK * lo : PACK * hi].rearrange("p (c i t) -> p c t i", i=4, t=PACK),
                in_=rows[:, :, lo:hi].rearrange("p t (c i) -> p c t i", i=4),
            )

        ident = keep.tile([P, P], F32, name="ident")
        vectors = keep.tile([P, KP], BF16, name="vectors")
        vector_words = vectors[:].bitcast(F32)
        half = P // 2
        nc.gpsimd.memset(vector_words[0:half, :], 0.0)
        make_identity(nc, ident[:])
        for u in range(2):
            nc.scalar.activation(
                out=vector_words[half:P, u * P : (u + 1) * P], in_=ident[half:P, :], func=ACT.Tanh, scale=0.0
            )

        j_raw, w_raw, s_raw, b_raw, m_raw = {}, {}, {}, {}, {}

        def load(src):
            staged = staging.tile(list(src.shape), BF16, name="staged")
            nc.sync.dma_start(out=staged[:], in_=src)
            return staged

        def load_joint(g, b):
            rows = joint[g * KP : (g + 1) * KP, :].rearrange("(m t) d -> m t d", t=PACK)
            j_raw[g, b] = load(rows[:, 2 * b : 2 * b + 2, :])

        def load_w(s):
            w_raw[s] = load(hidden_w[s * KP : (s + 1) * KP, :].rearrange("(p t) f -> p t f", t=PACK))

        def load_slopes(c, g):
            rows = slopes[g * KP : (g + 1) * KP, c * KP : (c + 1) * KP]
            s_raw[c, g] = load(rows.rearrange("(p t) v -> p t v", t=PACK))[:]

        def load_slopes_twice_as_wide(c, g):
            rows = slopes[g * KP : (g + 1) * KP, c * KP : (c + 2) * KP]
            staged = keep.tile([P, PACK, 2 * KP], BF16, name="wide%d" % g)
            nc.sync.dma_start(out=staged[:], in_=rows.rearrange("(p t) v -> p t v", t=PACK))
            for i in range(2):
                s_raw[c + i, g] = staged[:, :, i * KP : (i + 1) * KP]

        def load_pairs(tiles, src, j):
            c, b = divmod(j, 2)
            rows = src[2 * b * P : 2 * (b + 1) * P, c * KP : (c + 2) * KP]
            staged = load(rows.rearrange("(i p) v -> p i v", p=P))
            tiles[j] = staged[:, :, 0:KP]
            tiles[j + 2] = staged[:, :, KP : 2 * KP]

        w_codes = keep.tile([P, NS, F], U32, name="w_codes", align_bytes=64)
        w_scales = keep.tile([P, NS, F], U8, name="w_scales", align_bytes=64)
        h_codes = keep.tile([P, NG, F], U32, name="h_codes", align_bytes=64)
        h_scales = keep.tile([P, NG, F], U8, name="h_scales", align_bytes=64)
        y_scales = keep.tile([P, NC, F], U8, name="y_scales", align_bytes=64)
        pen_cols = keep.tile([P, PEN_ROWS], F32, name="pen_cols")
        w_grp, j_grp, j_codes, j_scales, tanh_a, h_grp = {}, {}, {}, {}, {}, {}

        def group_w(s):
            w_grp[s] = work.tile([P, PACK * F], BF16, name="w_grp", tag="grouped", bufs=3, align_bytes=64)
            interleave(nc.vector.tensor_copy, w_grp[s], w_raw[s][:], 0, W_VECTOR_COLS)
            interleave(nc.scalar.copy, w_grp[s], w_raw[s][:], W_VECTOR_COLS, F)

        def quantize_w(s):
            quantize(w_codes[:, s, :], w_scales[:, s, :], w_grp[s][:])

        def turn_joint(g, b):
            j_grp[g, b] = work.tile([P, 2, D], BF16, name="j_grp", align_bytes=64)
            for i in range(2):
                words = j_raw[g, b][:, i, :].bitcast(F32)
                turned = bank(JOINT_BANKS[(PACK * g + 2 * b + i) % len(JOINT_BANKS)], [P, 2 * NS, P])
                for s in range(NS):
                    for u in range(2):
                        every_second = words[:, 2 * P * s + u : 2 * P * (s + 1) : 2]
                        nc.tensor.transpose(turned[:, 2 * s + u, :], every_second, ident[:])
                nc.scalar.copy(
                    out=j_grp[g, b][:, i, :].bitcast(F32).rearrange("p (s m u) -> p s m u", s=NS, u=2),
                    in_=turned[:].rearrange("p (s u) m -> p s m u", u=2),
                )

        def quantize_joint(g, b):
            j_codes[g, b] = work.tile([P, 2 * NS * P], U32, name="j_codes", bufs=4, align_bytes=64)
            j_scales[g, b] = work.tile([P, 2 * NS * P], U8, name="j_scales", bufs=4, align_bytes=64)
            quantize(j_codes[g, b][:], j_scales[g, b][:], j_grp[g, b][:].rearrange("p i d -> p (i d)"))

        def hidden(g, b):
            tanh_a[g, b] = work.tile([P, 2, P, PACK], F32, name="tanh_a")
            for i in range(2):
                a = 2 * b + i
                acc = bank(HIDDEN_BANKS[(NF * g + a) % len(HIDDEN_BANKS)], [P, PACK, P])
                units = slice(a * P, (a + 1) * P)
                for t in range(PACK):
                    for s in range(NS):
                        first = (NS * (t % 2) + s) * P
                        nc.tensor.matmul_mx(
                            out=acc[:, t, :],
                            lhsT=j_codes[g, t // 2][:, first : first + P].bitcast(FP8X4),
                            lhsT_scale=j_scales[g, t // 2][:, first : first + P],
                            rhs=w_codes[:, s, units].bitcast(FP8X4),
                            rhs_scale=w_scales[:, s, units],
                            start=(s == 0),
                            stop=(s == NS - 1),
                        )
                nc.scalar.activation(
                    out=tanh_a[g, b][:, i, :, :], in_=acc[:].rearrange("m t f -> m f t"), func=ACT.Tanh
                )

        def weigh(g, b):
            if b == 0:
                h_grp[g] = work.tile([P, PACK * F], BF16, name="h_grp", align_bytes=64)
            row = PEN_ROWS + g
            weights = turned_vectors[:].bitcast(BF16)[:, 1:3, 2 * row : 2 * row + 2]
            nc.vector.tensor_tensor(
                out=h_grp[g][:, 2 * b * KP : 2 * (b + 1) * KP].rearrange("m (f u e) -> m f u e", u=2, e=2),
                in0=tanh_a[g, b][:].rearrange("m i f (u e) -> m (i f) u e", u=2),
                in1=weights.rearrange("m u (o e) -> m o u e", o=1).to_broadcast([P, 2 * P, 2, 2]),
                op=ALU.mult,
            )

        def quantize_h(g):
            quantize(h_codes[:, g, :], h_scales[:, g, :], h_grp[g][:])

        s_grp, s_codes, s_scales, pen, prod, rest = {}, {}, {}, {}, {}, {}
        g_acc, y, y_bf, y_turned, y_grp, y_codes = {}, {}, {}, {}, {}, {}

        def slopes_share(c, g):
            if (c, g) not in s_grp:
                single = (c, g) in GPSIMD_COLS or (c, g) == (0, 0)
                s_grp[c, g] = work.tile(
                    [P, PACK * KP],
                    BF16,
                    name="s_grp",
                    tag="single" if single else "grouped",
                    bufs=1 if single else 3,
                    align_bytes=64,
                )
            lo = GPSIMD_COLS.get((c, g), 0)
            return s_grp[c, g], lo, lo + VECTOR_COLS.get((c, g), 0)

        def group_on_gpsimd(c, g):
            grouped, lo, hi = slopes_share(c, g)
            nc.gpsimd.tensor_scalar(
                out=grouped[:, 0 : PACK * lo].rearrange("p (v t) -> p v t", t=PACK),
                in0=s_raw[c, g][:, :, 0:lo].rearrange("p t v -> p v t"),
                scalar1=1.0,
                scalar2=0.0,
                op0=ALU.mult,
                op1=ALU.add,
            )

        def group_on_vector(c, g):
            grouped, lo, hi = slopes_share(c, g)
            if hi > lo:
                interleave(nc.vector.tensor_copy, grouped, s_raw[c, g], lo, hi)

        def group_on_scalar(c, g):
            grouped, lo, hi = slopes_share(c, g)
            interleave(nc.scalar.copy, grouped, s_raw[c, g], hi, KP)

        def quantize_slopes(c, g):
            if g == 0:
                s_codes[c] = work.tile([P, NG, KP], U32, name="s_codes", align_bytes=64)
                s_scales[c] = work.tile([P, NG, KP], U8, name="s_scales", align_bytes=64)
            quantize(s_codes[c][:, g, :], s_scales[c][:, g, :], s_grp[c, g][:])

        def spread_penalty(h):
            pen[h] = bank(PENALTY_BANKS[h], [P, 4, P])
            for i in range(4):
                column = pen_cols[:, 4 * h + i : 4 * h + i + 1]
                nc.tensor.transpose(pen[h][:, i, :], column.to_broadcast([P, P]), ident[:])

        def penalty_term(j):
            c, b = divmod(j, 2)
            row = pen[c // 2][:].rearrange("p i w -> p (i w)").bitcast(BF16)[:, (c % 2) * KP : (c % 2 + 1) * KP]
            prod[j] = work.tile([P, 2, KP], F32, name="prod")
            nc.vector.tensor_tensor(
                out=prod[j][:],
                in0=b_raw[j],
                in1=row.rearrange("p (o v) -> p o v", o=1).to_broadcast([P, 2, KP]),
                op=ALU.mult,
            )

        def momentum_term(j):
            c, b = divmod(j, 2)
            rest[j] = work.tile([P, 2, KP], F32, name="rest", bufs=4)
            nc.vector.scalar_tensor_tensor(
                out=rest[j][:],
                in0=m_raw[j],
                scalar=BETA,
                in1=prod[j][:],
                op0=ALU.mult,
                op1=ALU.add,
            )

        def gradient(c, a, g):
            if g == 0:
                g_acc[c, a] = bank((GRADIENT_BANKS if c < NC - 1 else LAST_BANKS)[a], [P, KP])
            units = slice(a * P, (a + 1) * P)
            nc.tensor.matmul_mx(
                out=g_acc[c, a][:],
                lhsT=h_codes[:, g, units].bitcast(FP8X4),
                lhsT_scale=h_scales[:, g, units],
                rhs=s_codes[c][:, g, :].bitcast(FP8X4),
                rhs_scale=s_scales[c][:, g, :],
                start=(g == 0),
                stop=(g == NG - 1),
            )

        def gradient_pair(j):
            c, b = divmod(j, 2)
            for a in (2 * b, 2 * b + 1):
                for g in range(NG):
                    gradient(c, a, g)

        def finish(c, a):
            y[c, a] = work.tile([P, KP], F32, name="y", bufs=6)
            nc.vector.tensor_tensor(
                out=y[c, a][:], in0=g_acc[c, a][:], in1=rest[2 * c + a // 2][:, a % 2, :], op=ALU.add
            )
            nc.sync.dma_start(out=out_0[a * P : (a + 1) * P, c * KP : (c + 1) * KP], in_=y[c, a][:])

        def round_y(c, a, copy=nc.scalar.copy):
            y_bf[c, a] = work.tile([P, 2, P, 2], BF16, name="y_bf", bufs=4)
            copy(out=y_bf[c, a][:], in_=y[c, a][:].rearrange("f (p u e) -> f u p e", u=2, e=2))

        def turn_y_tile(c, a, turned):
            words = y_bf[c, a][:].rearrange("f u p e -> f (u p e)").bitcast(F32)
            for u in range(2):
                nc.tensor.transpose(turned[:, u, :], words[:, u * P : (u + 1) * P], ident[:])

        def turn_y(j):
            c, b = divmod(j, 2)
            y_turned[j] = bank(Y_BANKS[j % 2], [P, 4, P])
            for i in range(2):
                turn_y_tile(c, 2 * b + i, y_turned[j][:, 2 * i : 2 * i + 2, :])

        def group_y(j):
            c, b = divmod(j, 2)
            if b == 0:
                y_grp[c] = work.tile([P, PACK * F], BF16, name="y_grp", align_bytes=64)
            nc.scalar.copy(
                out=y_grp[c][:].bitcast(F32)[:, b * KP : (b + 1) * KP].rearrange("p (i f u) -> p i f u", i=2, u=2),
                in_=y_turned[j][:].rearrange("p (i u) f -> p i f u", u=2),
            )

        def turn_and_group_tile(c, a, copy):
            turned = bank(Y_BANKS[(a + 1) % 2], [P, 2, P])
            turn_y_tile(c, a, turned[:])
            copy(
                out=y_grp[c][:].bitcast(F32)[:, a * 2 * P : (a + 1) * 2 * P].rearrange("p (f u) -> p f u", u=2),
                in_=turned[:].rearrange("p u f -> p f u"),
            )

        def quantize_y(c, lo, hi):
            if lo == 0:
                y_codes[c] = work.tile([P, F], U32, name="y_codes", align_bytes=64)
            quantize(y_codes[c][:, lo:hi], y_scales[:, c, lo:hi], y_grp[c][:, PACK * lo : PACK * hi])
            words = out_1[c, :, :, :].rearrange("p f t -> p (f t)").bitcast(I32)
            nc.sync.dma_start(out=words[:, lo:hi], in_=y_codes[c][:, lo:hi].bitcast(I32))

        load_w(0)
        load_joint(0, 0)
        nc.sync.dma_start(out=vectors[0:PEN_ROWS, 0 : 2 * P], in_=penalty.rearrange("(i w) -> i w", w=2 * P))
        nc.sync.dma_start(out=vectors[PEN_ROWS : PEN_ROWS + NG, :], in_=state_w.rearrange("(g r) -> g r", r=KP))
        load_w(1)
        load_joint(0, 1)
        load_pairs(b_raw, bottleneck, 0)
        load_joint(1, 0)
        load_pairs(m_raw, momentum, 0)
        load_joint(1, 1)
        load_slopes(0, 0)
        load_joint(2, 0)
        load_slopes(0, 1)
        load_joint(2, 1)
        load_slopes(0, 2)
        load_joint(3, 0)
        load_joint(3, 1)
        load_slopes(0, 3)

        group_w(0)
        turn_joint(0, 0)
        turned_vectors = bank(STATE_BANK, [P, 3, P])
        nc.tensor.transpose(turned_vectors[:, 0, :], vector_words[:, 0:P], ident[:])
        for u in range(2):
            nc.tensor.transpose(turned_vectors[:, 1 + u, :], vector_words[:, u : 2 * P : 2], ident[:])
        nc.scalar.copy(out=pen_cols[:], in_=turned_vectors[:, 0, 0:PEN_ROWS])
        quantize_w(0)
        group_w(1)
        quantize_joint(0, 0)
        spread_penalty(0)
        turn_joint(0, 1)
        quantize_w(1)
        penalty_term(TERMS[0])
        quantize_joint(0, 1)

        last_g = NG - 1
        for g in range(NG):
            if g < last_g:
                turn_joint(g + 1, 0)
            else:
                spread_penalty(1)
            if g == 1:
                load_slopes(1, 0)
                load_slopes(1, 1)
                load_pairs(b_raw, bottleneck, 1)
                load_slopes(1, 2)
                load_pairs(m_raw, momentum, 1)
                load_slopes(1, 3)
            if g > 0:
                group_on_scalar(0, g)
            hidden(g, 0)
            if g == 0:
                penalty_term(TERMS[1])
                momentum_term(TERMS[0])
            else:
                if g == last_g:
                    penalty_term(TERMS[2])
                group_on_vector(0, g)
                quantize_h(g - 1)
            if g < last_g:
                quantize_joint(g + 1, 0)
                turn_joint(g + 1, 1)
            else:
                momentum_term(TERMS[2])
            hidden(g, 1)
            if g == 0:
                momentum_term(TERMS[1])
                group_on_vector(0, 0)
            if g == last_g - 1:
                group_on_scalar(1, 0)
            if g < last_g:
                quantize_joint(g + 1, 1)
            quantize_slopes(0, g)
            if g < last_g:
                group_on_gpsimd(0, g + 1)
            else:
                group_on_gpsimd(1, 1)
            weigh(g, 0)
            weigh(g, 1)
        load_slopes_twice_as_wide(2, 0)
        load_slopes_twice_as_wide(2, 1)
        load_pairs(b_raw, bottleneck, 4)
        load_slopes_twice_as_wide(2, 2)
        load_pairs(m_raw, momentum, 4)
        load_slopes_twice_as_wide(2, 3)
        group_on_scalar(1, 1)
        group_on_scalar(1, 2)
        quantize_slopes(1, 0)
        quantize_h(last_g)
        gradient_pair(0)

        last_full = 2 * NC - 4
        for j in range(last_full + 1):
            c, b = divmod(j, 2)
            if j > 0:
                quantize_slopes(c + 1, 2 * b)
                momentum_term(TERMS[j + 2])
            quantize_slopes(c + 1, 2 * b + 1)
            gradient_pair(j + 1)
            if j > 0:
                turn_y(j - 1)
            shared = ((j + 3) // 2, 2 * ((j + 3) % 2) + 1)
            group_on_gpsimd(*shared)
            group_on_scalar(*shared)
            penalty_term(TERMS[j + 3])
            if j < last_full:
                group_on_scalar(c + 2, 2 * b)
            if j > 0:
                group_y(j - 1)
            finish(c, 2 * b)
            finish(c, 2 * b + 1)
            if j == 0:
                load_pairs(b_raw, bottleneck, 5)
                load_pairs(m_raw, momentum, 5)
            round_y(c, 2 * b)
            round_y(c, 2 * b + 1)
            if j < last_full:
                group_on_vector(c + 2, 2 * b)
            if b == 1 and c > 0:
                quantize_y(c - 1, 0, F)

        c = NC - 1
        for a in range(NF):
            for g in range(2):
                gradient(c, a, g)
        quantize_slopes(c, 2)
        quantize_slopes(c, 3)
        for a in range(NF):
            gradient(c, a, 2)
        turn_y(2 * c - 2)
        for a in range(NF):
            gradient(c, a, 3)
        for a in (2, 3):
            finish(c - 1, a)
        for a in (2, 3):
            round_y(c - 1, a)
        group_y(2 * c - 2)
        momentum_term(TERMS[-1])
        quantize_y(c - 2, 0, F)
        turn_y(2 * c - 1)
        for a in range(NF):
            finish(c, a)
            if a < 2:
                round_y(c, a)
        group_y(2 * c - 1)
        turn_y(2 * c)
        group_y(2 * c)
        for a in (2, 3):
            round_y(c, a, nc.vector.tensor_copy)
        quantize_y(c - 1, 0, F)
        quantize_y(c, 0, F // 2)
        turn_and_group_tile(c, 2, nc.scalar.copy)
        turn_and_group_tile(c, 3, nc.vector.tensor_copy)
        quantize_y(c, F // 2, F)

        for q in range(4):
            queue = nc.sync if q < 2 else nc.scalar
            queue.dma_start(
                out=out_2[:, 4 * q : 4 * q + 4, :].rearrange("c r f -> r c f").bitcast(I32),
                in_=y_scales[32 * q : 32 * q + 4, :, :].bitcast(I32),
            )
